import numpy as np
import ml_dtypes


def mxq(x, axis, fmt="e4m3"):
    dtype, down = {"e4m3": (ml_dtypes.float8_e4m3fn, 7), "e5m2": (ml_dtypes.float8_e5m2, 14)}[fmt]
    v = np.moveaxis(np.asarray(x, np.float32).astype(ml_dtypes.bfloat16).astype(np.float64), axis, -1)
    blocks = v.reshape(v.shape[:-1] + (-1, 32))
    amax = np.abs(blocks).max(-1, keepdims=True)
    byte = np.maximum(np.where(amax > 0, np.frexp(amax)[1] - 1 + 127, 0) - down, 1)
    scale = np.exp2(byte - 127.0)
    codes = (blocks / scale).astype(np.float32).astype(dtype).astype(np.float64)
    return np.moveaxis((codes * scale).reshape(v.shape), -1, axis)


WIDE = False


def mx_kscale(k):
    if not WIDE:
        return np.ones(k)
    levels = np.array([10, -10, 5, -5, 0])
    if k % 512:
        return np.exp2(np.random.permutation(np.resize(levels, k // 32))).repeat(32)
    a = np.empty((k // 512, 16))
    for p in range(k // 512):
        a[p, :8] = np.random.permutation(np.resize(levels, 8))
        for g in range(8):
            far = levels[np.abs(levels - a[p, g]) >= 10]
            a[p, g + 8] = far[np.random.randint(len(far))]
    return np.exp2(a.ravel()).repeat(32)


def f64(x):
    return np.asarray(x).astype(np.float64)


def striped(idx):
    return np.tile(idx.reshape(-1, 16).T, (8, 1)).astype(np.uint16)


def unstriped(offs):
    return offs[:16].T.reshape(-1).astype(np.int64)


E2M1 = np.array([0.0, 0.5, 1.0, 1.5, 2.0, 3.0, 4.0, 6.0, -0.0, -0.5, -1.0, -1.5, -2.0, -3.0, -4.0, -6.0])


def pack_weight(w, fmt):
    k, n = w.shape
    w = f64(np.asarray(w, np.float32).astype(ml_dtypes.bfloat16)).reshape(k // 32, 32, n)
    amax = np.abs(w).max(1)
    if fmt == "e4m3":
        byte = np.frexp(amax)[1] - 1 + 127 - 7
    else:
        mant, ex = np.frexp(amax / 6.0)
        byte = np.where(mant > 0.5, ex, ex - 1) + 127
    byte = np.clip(np.where(amax > 0, byte, 1), 1, 254)
    scaled = (w * np.exp2(127.0 - byte)[:, None, :]).reshape(k, n).astype(np.float32)
    by_word = np.ascontiguousarray(scaled.reshape(k // 512, 128, 4, n).transpose(0, 1, 3, 2))
    if fmt == "e4m3":
        words = by_word.astype(ml_dtypes.float8_e4m3fn).view(np.uint8)
    else:
        c = by_word.astype(ml_dtypes.float4_e2m1fn).view(np.uint8) & 0xF
        words = (c[..., 0::2] | (c[..., 1::2] << 4)).reshape(k // 512, 128, 2 * n)
    return np.ascontiguousarray(words), np.ascontiguousarray(byte.astype(np.uint8).reshape(k // 512, 16, n))


def unpack_weight(words, scales, fmt):
    g, _, n = scales.shape
    words = np.ascontiguousarray(words).reshape(g, 128, n, -1)
    if fmt == "e4m3":
        vals = words.view(ml_dtypes.float8_e4m3fn).astype(np.float64)
    else:
        nib = np.empty((g, 128, n, 4), np.uint8)
        nib[..., 0::2] = words & 0xF
        nib[..., 1::2] = words >> 4
        vals = E2M1[nib]
    vals = vals * np.repeat(np.exp2(scales.astype(np.float64) - 127.0), 8, axis=1)[..., None]
    return vals.transpose(0, 1, 3, 2).reshape(g * 512, n)


def relu2(v):
    return np.maximum(v, 0.0) ** 2


K, T, E, C, H, N, TOP = 1536, 512, 6, 256, 512, 128, 3


def by_expert(wq, xq):
    return np.concatenate([wq[e].T @ xq[:, e * C:(e + 1) * C] for e in range(E)], axis=1)


def setup_inputs():
    n = np.random.standard_normal
    s = mx_kscale(K)
    u = mx_kscale(H)
    deal = np.repeat(np.arange(E), C).reshape(TOP, T)[:, np.random.permutation(T)]
    deal = np.take_along_axis(deal, np.argsort(np.random.rand(TOP, T), axis=0), axis=0)
    for _ in range(8):
        s_, t_ = np.random.permutation(T).reshape(2, -1); r = np.random.randint(TOP, size=T // 2); x, y = deal[r, s_].copy(), deal[r, t_].copy()
        ok = ~((deal[:, s_] == y).any(0) | (deal[:, t_] == x).any(0)); deal[r[ok], s_[ok]] = y[ok]; deal[r[ok], t_[ok]] = x[ok]
    order = np.lexsort((np.random.rand(TOP * T), deal.reshape(-1)))
    slot_token = order % T; pos = np.empty(TOP * T, np.int64); pos[order] = np.arange(TOP * T); pos = pos.reshape(TOP, T)
    g = np.random.uniform(0.5, 1.5, (TOP, T)); g = g / g.sum(0)
    x = pack_weight(n((K, T)) * s[:, None], "e4m3")
    return {
        "x_words": x[0],
        "x_scales": x[1],
        "w": (n((K, N)) / np.sqrt(K) / s[:, None]).astype(np.float32),
        "wa": (n((E, K, H)) / np.sqrt(K) / s[None, :, None] * u).astype(np.float32),
        "wb": (n((E, H, N)) / np.sqrt(H) / u[None, :, None] ** 2).astype(np.float32),
        "gate": np.stack([np.tile(r, (128, 1)) for r in g]).astype(np.float32),
        "offs": striped(slot_token),
        "pos1": striped(pos[0]),
        "pos2": striped(pos[1]),
        "pos3": striped(pos[2]),
    }


def reference(x_words, x_scales, w, wa, wb, gate, offs, pos1, pos2, pos3):
    wq = mxq(f64(w), 0, "e4m3")
    waq = mxq(f64(wa), 1, "e4m3")
    wbq = mxq(f64(wb), 1, "e4m3")
    idx = unstriped(offs)
    x = unpack_weight(x_words, x_scales, "e4m3")
    base = wq.T @ x
    h = relu2(by_expert(waq, x[:, idx]))
    y = by_expert(wbq, mxq(h, 0, "e4m3"))
    c = sum(f64(gate[r, :1]) * y[:, unstriped(p)] for r, p in enumerate((pos1, pos2, pos3)))
    return base + c

@@ -1,0 +1,232 @@
+from contextlib import ExitStack
+
+import concourse.mybir as mybir
+
+K, T, E, C, H, N, TOP = 1536, 512, 6, 256, 512, 128, 3
+P = 128
+PACK = 4
+K_PASS = P * PACK
+PASSES = K // K_PASS
+SLOTS = E * C
+
+FLOPS = 2 * K * N * T + 2 * SLOTS * K * H + 2 * SLOTS * H * N
+
+F32 = mybir.dt.float32
+BF16 = mybir.dt.bfloat16
+I32 = mybir.dt.int32
+U32 = mybir.dt.uint32
+U16 = mybir.dt.uint16
+U8 = mybir.dt.uint8
+FP8X4 = mybir.dt.float8_e4m3fn_x4
+MULT = mybir.AluOpType.mult
+ADD = mybir.AluOpType.add
+RELU = mybir.ActivationFunctionType.Relu
+SQUARE = mybir.ActivationFunctionType.Square
+
+SCALAR_SHARE = 64
+RAW_SLOTS = 14
+WORD_SLOTS = 5
+GATHER_AHEAD = 3
+GROUP_SLOTS = 4
+H_BANKS = 6
+CHUNKS = E * PASSES
+MAX = mybir.AluOpType.max
+
+
+def tile_moe_adp_relu2_kernel(
+    tc, x_words, x_scales, w, wa, wb, gate, offs, pos1, pos2, pos3, out
+):
+    nc = tc.nc
+    with ExitStack() as ctx:
+        keep = ctx.enter_context(tc.tile_pool(name="keep", bufs=1))
+        ring = ctx.enter_context(tc.tile_pool(name="ring", bufs=1))
+        psum = ctx.enter_context(tc.psum_pool(name="psum", bufs=1))
+
+        slot_tokens = keep.tile([P, SLOTS // 16], U16, name="slot_tokens")
+        nc.sync.dma_start(slot_tokens[:], offs)
+
+        token_scales = keep.tile([P, T], U8, name="token_scales", align_bytes=64)
+        nc.vector.memset(token_scales[:].bitcast(I32), 0)
+
+        token_words = [keep.tile([P, T], I32, name="token_words%d" % s, align_bytes=64) for s in range(PASSES)]
+        slot_results = keep.tile([P, SLOTS], F32, name="slot_results", align_bytes=64)
+
+        loaded = []
+
+        def load(shape, source):
+            tag = "raw%d" % (len(loaded) % RAW_SLOTS)
+            raw = ring.tile(shape, F32, name=tag, align_bytes=64)
+            nc.sync.dma_start(out=raw[:], in_=source)
+            loaded.append(tag)
+            return raw
+
+        def load_rows(rows):
+            return load([P, PACK, rows.shape[1]], rows.rearrange("(p j) c -> p j c", j=PACK))
+
+        def load_words(s):
+            nc.sync.dma_start(
+                out=token_words[s][:],
+                in_=x_words[s].rearrange("p t d -> p (t d)").bitcast(I32),
+            )
+
+        def quantize(grouped, width, name, codes_tag=None):
+            codes = ring.tile([P, width], U32, name=codes_tag or name + "_codes", align_bytes=64)
+            scales = ring.tile([P, width], U8, name=name + "_scales", align_bytes=64)
+            nc.vector.quantize_mx(out=codes[:].bitcast(FP8X4), scales=scales[:], in_=grouped[:])
+            return codes, scales
+
+        def interleaved(grouped, raw):
+            dst = grouped[:].rearrange("p (c i j) -> p c j i", i=4, j=PACK)
+            src = raw.rearrange("p j (c i) -> p c j i", i=4)
+            return dst, src
+
+        slot_words = {}
+        slot_scales = {}
+
+        def gather(chunk):
+            e, s = divmod(chunk, PASSES)
+            offsets = slot_tokens[:, e * C // 16 : (e + 1) * C // 16]
+            if s == 0:
+                slot_scales[e] = ring.tile([P, C], U8, name="slot_scales%d" % (e % 2), align_bytes=64)
+                nc.vector.tensor_copy(slot_scales[e][:], token_scales[:].indirect(offsets))
+            slot_words[chunk] = ring.tile([P, C], U32, name="slot_words%d" % (chunk % WORD_SLOTS), align_bytes=64)
+            nc.vector.tensor_copy(slot_words[chunk][:], token_words[s][:].bitcast(U32).indirect(offsets))
+
+        h_banks = {}
+        positive = {}
+        h_grouped = {}
+        wb_mx = {}
+
+        def prepare_wb(e):
+            wb_raw = load_rows(wb[e])
+            wb_grouped = ring.tile([P, PACK * N], BF16, name="wb_grouped%d" % (e % 2), align_bytes=64)
+            dst, src = interleaved(wb_grouped, wb_raw[:])
+            nc.vector.tensor_copy(out=dst, in_=src)
+            wb_mx[e] = quantize(wb_grouped, N, "wb%d" % (e % 2))
+
+        def rectify(e, tag):
+            positive[e] = ring.tile([P, PACK, C], F32, name=tag, align_bytes=64)
+            for t in range(PACK):
+                if e == E - 1 and t % 2 == 1:
+                    nc.vector.tensor_scalar(positive[e][:, t, :], h_banks[e][t][:], 0.0, None, MAX)
+                else:
+                    nc.scalar.activation(out=positive[e][:, t, :], in_=h_banks[e][t][:], func=RELU)
+
+        def square(e, tag):
+            h_grouped[e] = ring.tile([P, PACK * C], BF16, name=tag, align_bytes=64)
+            dst, src = interleaved(h_grouped[e], positive[e][:])
+            if e == E - 1:
+                half = C // 8
+                nc.scalar.activation(out=dst[:, :half], in_=src[:, :half], func=SQUARE)
+                nc.vector.tensor_tensor(dst[:, half:], src[:, half:], src[:, half:], MULT)
+            else:
+                nc.scalar.activation(out=dst, in_=src, func=SQUARE)
+
+        def second_layer(e, tag):
+            h_codes, h_scales = quantize(h_grouped[e], C, "h%d" % (e % 2), tag)
+            wb_codes, wb_scales = wb_mx[e]
+            y_bank = psum.tile([P, C], F32, name="y_bank")
+            nc.tensor.matmul_mx(
+                out=y_bank[:],
+                lhsT=wb_codes[:].bitcast(FP8X4),
+                lhsT_scale=wb_scales[:],
+                rhs=h_codes[:].bitcast(FP8X4),
+                rhs_scale=h_scales[:],
+                start=True,
+                stop=True,
+            )
+            nc.scalar.copy(out=slot_results[:, e * C : (e + 1) * C], in_=y_bank[:])
+
+        load_words(0)
+        wa_first = load_rows(wa[0, :K_PASS, :])
+        for q in range(4):
+            nc.sync.dma_start(
+                out=token_scales[32 * q : 32 * q + 4 * PASSES, :].bitcast(I32),
+                in_=x_scales[:, 4 * q : 4 * q + 4, :].bitcast(I32),
+            )
+        load_words(1)
+        load_words(2)
+        for chunk in range(GATHER_AHEAD):
+            gather(chunk)
+
+        for chunk in range(CHUNKS):
+            e, s = divmod(chunk, PASSES)
+            if chunk == 0:
+                wa_raw = wa_first
+            else:
+                wa_raw = load_rows(wa[e, s * K_PASS : (s + 1) * K_PASS, :])
+            freed_tag = loaded[-1]
+            if s == 0:
+                h_banks[e] = [
+                    psum.tile([P, C], F32, name="h_bank%d" % ((PACK * e + t) % H_BANKS)) for t in range(PACK)
+                ]
+            wa_grouped = ring.tile([P, PACK * H], BF16, name="wa_grouped%d" % (chunk % GROUP_SLOTS), align_bytes=64)
+            dst = wa_grouped[:].rearrange("p (t m j) -> p m j t", t=PACK, j=PACK)
+            src = wa_raw[:].rearrange("p j (m t) -> p m j t", t=PACK)
+            nc.scalar.copy(out=dst[:, :SCALAR_SHARE], in_=src[:, :SCALAR_SHARE])
+            nc.vector.tensor_copy(out=dst[:, SCALAR_SHARE:], in_=src[:, SCALAR_SHARE:])
+            if chunk + GATHER_AHEAD < CHUNKS:
+                gather(chunk + GATHER_AHEAD)
+            wa_codes, wa_scales = quantize(wa_grouped, H, "wa%d" % (chunk % GROUP_SLOTS))
+            if e > 0 and s == 0:
+                rectify(e - 1, freed_tag)
+            for t in range(PACK):
+                cols = slice(t * P, (t + 1) * P)
+                nc.tensor.matmul_mx(
+                    out=h_banks[e][t][:],
+                    lhsT=wa_codes[:, cols].bitcast(FP8X4),
+                    lhsT_scale=wa_scales[:, cols],
+                    rhs=slot_words[chunk][:].bitcast(FP8X4),
+                    rhs_scale=slot_scales[e][4 * s : P, :],
+                    start=(s == 0),
+                    stop=(s == PASSES - 1),
+                )
+            if e > 0 and s == 0:
+                prepare_wb(e - 1)
+            if e > 0 and s == 1:
+                square(e - 1, freed_tag)
+            if e > 0 and s == 2:
+                second_layer(e - 1, freed_tag)
+
+        token_slots = []
+        for r, pos in enumerate((pos1, pos2, pos3)):
+            slots = keep.tile([P, T // 16], U16, name="token_slots%d" % r)
+            nc.sync.dma_start(slots[:], pos)
+            token_slots.append(slots)
+
+        prepare_wb(E - 1)
+        rectify(E - 1, "last_positive")
+        square(E - 1, "last_h_grouped")
+        second_layer(E - 1, "last_h_codes")
+
+        gates = load([P, TOP, T], gate.rearrange("r p t -> p r t"))
+        w_raw = load([P, PASSES, PACK, N], w.rearrange("(s p j) n -> p s j n", p=P, j=PACK))
+
+        base_bank = psum.tile([P, T], F32, name="base_bank")
+        for s in range(PASSES):
+            w_grouped = keep.tile([P, PACK * N], BF16, name="w_grouped%d" % s, align_bytes=64)
+            dst, src = interleaved(w_grouped, w_raw[:, s])
+            nc.scalar.copy(out=dst, in_=src)
+            w_codes, w_scales = quantize(w_grouped, N, "w%d" % s)
+            nc.tensor.matmul_mx(
+                out=base_bank[:],
+                lhsT=w_codes[:].bitcast(FP8X4),
+                lhsT_scale=w_scales[:],
+                rhs=token_words[s][:].bitcast(FP8X4),
+                rhs_scale=token_scales[4 * s : P, :],
+                start=(s == 0),
+                stop=(s == PASSES - 1),
+            )
+
+        terms = []
+        for r in range(TOP):
+            term = keep.tile([P, T], F32, name="term%d" % r)
+            nc.vector.tensor_tensor(term[:], slot_results[:].indirect(token_slots[r][:]), gates[:, r, :], MULT)
+            terms.append(term)
+        first = keep.tile([P, T], F32, name="first")
+        second = keep.tile([P, T], F32, name="second")
+        total = keep.tile([P, T], F32, name="total")
+        nc.vector.tensor_tensor(first[:], terms[0][:], terms[1][:], ADD)
+        nc.vector.tensor_tensor(second[:], terms[2][:], base_bank[:], ADD)
+        nc.vector.tensor_tensor(total[:], first[:], second[:], ADD)
+        nc.sync.dma_start(out=out, in_=total[:])

@@ -23,9 +23,9 @@ ADD = mybir.AluOpType.add
 RELU = mybir.ActivationFunctionType.Relu
 SQUARE = mybir.ActivationFunctionType.Square
 
-SCALAR_SHARE = 64
+CAST_ENGINES = ["SS", "SS", "SV"] + ["SS", "VV", "SV"] * (E - 1)
 RAW_SLOTS = 14
-WORD_SLOTS = 5
+WORD_SLOTS = 6
 GATHER_AHEAD = 3
 GROUP_SLOTS = 4
 H_BANKS = 6
@@ -97,12 +97,19 @@ def tile_moe_adp_relu2_kernel(
         h_grouped = {}
         wb_mx = {}
 
-        def prepare_wb(e):
-            wb_raw = load_rows(wb[e])
-            wb_grouped = ring.tile([P, PACK * N], BF16, name="wb_grouped%d" % (e % 2), align_bytes=64)
-            dst, src = interleaved(wb_grouped, wb_raw[:])
+        wb_raw = {}
+        wb_grouped = {}
+
+        def load_wb(e):
+            wb_raw[e] = load_rows(wb[e])
+
+        def round_wb(e):
+            wb_grouped[e] = ring.tile([P, PACK * N], BF16, name="wb_grouped%d" % (e % 2), align_bytes=64)
+            dst, src = interleaved(wb_grouped[e], wb_raw[e][:])
             nc.vector.tensor_copy(out=dst, in_=src)
-            wb_mx[e] = quantize(wb_grouped, N, "wb%d" % (e % 2))
+
+        def quantize_wb(e):
+            wb_mx[e] = quantize(wb_grouped[e], N, "wb%d" % (e % 3))
 
         def rectify(e, tag):
             positive[e] = ring.tile([P, PACK, C], F32, name=tag, align_bytes=64)
@@ -122,10 +129,15 @@ def tile_moe_adp_relu2_kernel(
             else:
                 nc.scalar.activation(out=dst, in_=src, func=SQUARE)
 
-        def second_layer(e, tag):
-            h_codes, h_scales = quantize(h_grouped[e], C, "h%d" % (e % 2), tag)
+        h_mx = {}
+
+        def quantize_h(e):
+            h_mx[e] = quantize(h_grouped[e], C, "h%d" % (e % 3))
+
+        def second_layer(e, bank_tag):
+            h_codes, h_scales = h_mx[e]
             wb_codes, wb_scales = wb_mx[e]
-            y_bank = psum.tile([P, C], F32, name="y_bank")
+            y_bank = psum.tile([P, C], F32, name=bank_tag)
             nc.tensor.matmul_mx(
                 out=y_bank[:],
                 lhsT=wb_codes[:].bitcast(FP8X4),
@@ -146,7 +158,7 @@ def tile_moe_adp_relu2_kernel(
             )
         load_words(1)
         load_words(2)
-        for chunk in range(GATHER_AHEAD):
+        for chunk in range(PASSES):
             gather(chunk)
 
         for chunk in range(CHUNKS):
@@ -155,21 +167,36 @@ def tile_moe_adp_relu2_kernel(
                 wa_raw = wa_first
             else:
                 wa_raw = load_rows(wa[e, s * K_PASS : (s + 1) * K_PASS, :])
-            freed_tag = loaded[-1]
-            if s == 0:
-                h_banks[e] = [
-                    psum.tile([P, C], F32, name="h_bank%d" % ((PACK * e + t) % H_BANKS)) for t in range(PACK)
-                ]
+            raw_tag = loaded[-1]
             wa_grouped = ring.tile([P, PACK * H], BF16, name="wa_grouped%d" % (chunk % GROUP_SLOTS), align_bytes=64)
             dst = wa_grouped[:].rearrange("p (t m j) -> p m j t", t=PACK, j=PACK)
             src = wa_raw[:].rearrange("p j (m t) -> p m j t", t=PACK)
-            nc.scalar.copy(out=dst[:, :SCALAR_SHARE], in_=src[:, :SCALAR_SHARE])
-            nc.vector.tensor_copy(out=dst[:, SCALAR_SHARE:], in_=src[:, SCALAR_SHARE:])
-            if chunk + GATHER_AHEAD < CHUNKS:
-                gather(chunk + GATHER_AHEAD)
+            for half, engine in enumerate(CAST_ENGINES[chunk]):
+                pair = slice(2 * half, 2 * half + 2)
+                if engine == "S":
+                    nc.scalar.copy(out=dst[:, :, :, pair], in_=src[:, :, :, pair])
+                else:
+                    nc.vector.tensor_copy(out=dst[:, :, :, pair], in_=src[:, :, :, pair])
+            if s == 0 and e + 1 < E:
+                for ahead in range(PASSES):
+                    gather(chunk + PASSES + ahead)
+            if s == 1 and e > 0:
+                round_wb(e - 1)
+            if s == 2 and e > 0:
+                quantize_wb(e - 1)
+                quantize_h(e - 1)
             wa_codes, wa_scales = quantize(wa_grouped, H, "wa%d" % (chunk % GROUP_SLOTS))
-            if e > 0 and s == 0:
-                rectify(e - 1, freed_tag)
+            if s == 0:
+                if e > 0:
+                    rectify(e - 1, raw_tag)
+                if e > 1:
+                    second_layer(e - 2, "h_bank%d" % (PACK * (e - 1) % H_BANKS))
+                if e > 0:
+                    square(e - 1, "h_grouped%d" % (e % 2))
+                    load_wb(e - 1)
+                h_banks[e] = [
+                    psum.tile([P, C], F32, name="h_bank%d" % ((PACK * e + t) % H_BANKS)) for t in range(PACK)
+                ]
             for t in range(PACK):
                 cols = slice(t * P, (t + 1) * P)
                 nc.tensor.matmul_mx(
@@ -181,12 +208,8 @@ def tile_moe_adp_relu2_kernel(
                     start=(s == 0),
                     stop=(s == PASSES - 1),
                 )
-            if e > 0 and s == 0:
-                prepare_wb(e - 1)
-            if e > 0 and s == 1:
-                square(e - 1, freed_tag)
-            if e > 0 and s == 2:
-                second_layer(e - 1, freed_tag)
+
+        second_layer(E - 2, "y_bank")
 
         token_slots = []
         for r, pos in enumerate((pos1, pos2, pos3)):
@@ -194,19 +217,25 @@ def tile_moe_adp_relu2_kernel(
             nc.sync.dma_start(slots[:], pos)
             token_slots.append(slots)
 
-        prepare_wb(E - 1)
+        w_raw = [load_rows(w[s * K_PASS : (s + 1) * K_PASS, :]) for s in range(PASSES)]
+        load_wb(E - 1)
+        gates = load([P, TOP, T], gate.rearrange("r p t -> p r t"))
+
         rectify(E - 1, "last_positive")
         square(E - 1, "last_h_grouped")
-        second_layer(E - 1, "last_h_codes")
-
-        gates = load([P, TOP, T], gate.rearrange("r p t -> p r t"))
-        w_raw = load([P, PASSES, PACK, N], w.rearrange("(s p j) n -> p s j n", p=P, j=PACK))
+        round_wb(E - 1)
+        quantize_h(E - 1)
+        quantize_wb(E - 1)
+        second_layer(E - 1, "y_bank")
 
         base_bank = psum.tile([P, T], F32, name="base_bank")
         for s in range(PASSES):
             w_grouped = keep.tile([P, PACK * N], BF16, name="w_grouped%d" % s, align_bytes=64)
-            dst, src = interleaved(w_grouped, w_raw[:, s])
-            nc.scalar.copy(out=dst, in_=src)
+            dst, src = interleaved(w_grouped, w_raw[s][:])
+            if s == 0:
+                nc.scalar.copy(out=dst, in_=src)
+            else:
+                nc.vector.tensor_copy(out=dst, in_=src)
             w_codes, w_scales = quantize(w_grouped, N, "w%d" % s)
             nc.tensor.matmul_mx(
                 out=base_bank[:],

@@ -23,7 +23,7 @@ ADD = mybir.AluOpType.add
 RELU = mybir.ActivationFunctionType.Relu
 SQUARE = mybir.ActivationFunctionType.Square
 
-CAST_ENGINES = ["SS", "SS", "SV"] + ["SS", "VV", "SV"] * (E - 1)
+CAST_ENGINES = ["SS", "SS", "SS", "SS", "SV", "SV"] + ["SS", "VV", "SV"] * 2 + ["SV", "VV", "SV"] * 2
 RAW_SLOTS = 14
 WORD_SLOTS = 6
 GATHER_AHEAD = 3
@@ -75,6 +75,12 @@ def tile_moe_adp_relu2_kernel(
             nc.vector.quantize_mx(out=codes[:].bitcast(FP8X4), scales=scales[:], in_=grouped[:])
             return codes, scales
 
+        def round_to_bf16(engine, dst, src):
+            if engine == "S":
+                nc.scalar.copy(out=dst, in_=src)
+            else:
+                nc.vector.tensor_copy(out=dst, in_=src)
+
         def interleaved(grouped, raw):
             dst = grouped[:].rearrange("p (c i j) -> p c j i", i=4, j=PACK)
             src = raw.rearrange("p j (c i) -> p c j i", i=4)
@@ -83,14 +89,13 @@ def tile_moe_adp_relu2_kernel(
         slot_words = {}
         slot_scales = {}
 
-        def gather(chunk):
-            e, s = divmod(chunk, PASSES)
+        def gather(e):
             offsets = slot_tokens[:, e * C // 16 : (e + 1) * C // 16]
-            if s == 0:
-                slot_scales[e] = ring.tile([P, C], U8, name="slot_scales%d" % (e % 2), align_bytes=64)
-                nc.vector.tensor_copy(slot_scales[e][:], token_scales[:].indirect(offsets))
-            slot_words[chunk] = ring.tile([P, C], U32, name="slot_words%d" % (chunk % WORD_SLOTS), align_bytes=64)
-            nc.vector.tensor_copy(slot_words[chunk][:], token_words[s][:].bitcast(U32).indirect(offsets))
+            slot_words[e] = ring.tile([P, PASSES, C], U32, name="last_grouped%d" % ((e + 1) % 4), align_bytes=64)
+            for s in range(PASSES):
+                nc.vector.tensor_copy(slot_words[e][:, s, :], token_words[s][:].bitcast(U32).indirect(offsets))
+            slot_scales[e] = ring.tile([P, C], U8, name="h_grouped%d" % (e % 4), align_bytes=64)
+            nc.vector.tensor_copy(slot_scales[e][:], token_scales[:].indirect(offsets))
 
         h_banks = {}
         positive = {}
@@ -103,10 +108,10 @@ def tile_moe_adp_relu2_kernel(
         def load_wb(e):
             wb_raw[e] = load_rows(wb[e])
 
-        def round_wb(e):
+        def round_wb(e, engine):
             wb_grouped[e] = ring.tile([P, PACK * N], BF16, name="wb_grouped%d" % (e % 2), align_bytes=64)
             dst, src = interleaved(wb_grouped[e], wb_raw[e][:])
-            nc.vector.tensor_copy(out=dst, in_=src)
+            round_to_bf16(engine, dst, src)
 
         def quantize_wb(e):
             wb_mx[e] = quantize(wb_grouped[e], N, "wb%d" % (e % 3))
@@ -149,26 +154,25 @@ def tile_moe_adp_relu2_kernel(
             )
             nc.scalar.copy(out=slot_results[:, e * C : (e + 1) * C], in_=y_bank[:])
 
-        load_words(0)
-        wa_first = load_rows(wa[0, :K_PASS, :])
+        for s in range(PASSES):
+            load_words(s)
         for q in range(4):
-            nc.sync.dma_start(
+            nc.scalar.dma_start(
                 out=token_scales[32 * q : 32 * q + 4 * PASSES, :].bitcast(I32),
                 in_=x_scales[:, 4 * q : 4 * q + 4, :].bitcast(I32),
             )
-        load_words(1)
-        load_words(2)
-        for chunk in range(PASSES):
-            gather(chunk)
+        gather(0)
+        gather(1)
 
-        for chunk in range(CHUNKS):
+        for chunk in range(CHUNKS - 1):
             e, s = divmod(chunk, PASSES)
-            if chunk == 0:
-                wa_raw = wa_first
-            else:
-                wa_raw = load_rows(wa[e, s * K_PASS : (s + 1) * K_PASS, :])
+            wa_raw = load_rows(wa[e, s * K_PASS : (s + 1) * K_PASS, :])
             raw_tag = loaded[-1]
-            wa_grouped = ring.tile([P, PACK * H], BF16, name="wa_grouped%d" % (chunk % GROUP_SLOTS), align_bytes=64)
+            if s == PASSES - 1:
+                grouped_tag = "last_grouped%d" % (e % 4)
+            else:
+                grouped_tag = "wa_grouped%d_%d" % (s, e % 2)
+            wa_grouped = ring.tile([P, PACK * H], BF16, name=grouped_tag, align_bytes=64)
             dst = wa_grouped[:].rearrange("p (t m j) -> p m j t", t=PACK, j=PACK)
             src = wa_raw[:].rearrange("p j (m t) -> p m j t", t=PACK)
             for half, engine in enumerate(CAST_ENGINES[chunk]):
@@ -177,11 +181,10 @@ def tile_moe_adp_relu2_kernel(
                     nc.scalar.copy(out=dst[:, :, :, pair], in_=src[:, :, :, pair])
                 else:
                     nc.vector.tensor_copy(out=dst[:, :, :, pair], in_=src[:, :, :, pair])
-            if s == 0 and e + 1 < E:
-                for ahead in range(PASSES):
-                    gather(chunk + PASSES + ahead)
-            if s == 1 and e > 0:
-                round_wb(e - 1)
+            if s == 0 and e + 2 < E:
+                gather(e + 2)
+            if s == 1 and 0 < e < E - 1:
+                round_wb(e - 1, "V")
             if s == 2 and e > 0:
                 quantize_wb(e - 1)
                 quantize_h(e - 1)
@@ -192,7 +195,8 @@ def tile_moe_adp_relu2_kernel(
                 if e > 1:
                     second_layer(e - 2, "h_bank%d" % (PACK * (e - 1) % H_BANKS))
                 if e > 0:
-                    square(e - 1, "h_grouped%d" % (e % 2))
+                    square(e - 1, "h_grouped%d" % ((e - 1) % 4))
+                if 0 < e < E - 1:
                     load_wb(e - 1)
                 h_banks[e] = [
                     psum.tile([P, C], F32, name="h_bank%d" % ((PACK * e + t) % H_BANKS)) for t in range(PACK)
@@ -203,13 +207,37 @@ def tile_moe_adp_relu2_kernel(
                     out=h_banks[e][t][:],
                     lhsT=wa_codes[:, cols].bitcast(FP8X4),
                     lhsT_scale=wa_scales[:, cols],
-                    rhs=slot_words[chunk][:].bitcast(FP8X4),
+                    rhs=slot_words[e][:, s, :].bitcast(FP8X4),
                     rhs_scale=slot_scales[e][4 * s : P, :],
                     start=(s == 0),
                     stop=(s == PASSES - 1),
                 )
 
-        second_layer(E - 2, "y_bank")
+        e, s = E - 1, PASSES - 1
+        pair_grouped = [
+            ring.tile([P, 2 * H], BF16, name="pair_grouped%d" % pair, align_bytes=64) for pair in range(2)
+        ]
+        for half in range(2):
+            wa_raw = load_rows(wa[e, s * K_PASS : (s + 1) * K_PASS, half * H // 2 : (half + 1) * H // 2])
+            src = wa_raw[:].rearrange("p j (m t) -> p m j t", t=PACK)
+            for pair, engine in enumerate("VS"):
+                dst = pair_grouped[pair][:].rearrange("p (t m j) -> p m j t", t=2, j=PACK)
+                round_to_bf16(
+                    engine, dst[:, half * P // 2 : (half + 1) * P // 2], src[:, :, :, 2 * pair : 2 * pair + 2]
+                )
+        for pair in range(2):
+            wa_codes, wa_scales = quantize(pair_grouped[pair], 2 * P, "pair%d" % pair)
+            for t in range(2):
+                cols = slice(t * P, (t + 1) * P)
+                nc.tensor.matmul_mx(
+                    out=h_banks[e][2 * pair + t][:],
+                    lhsT=wa_codes[:, cols].bitcast(FP8X4),
+                    lhsT_scale=wa_scales[:, cols],
+                    rhs=slot_words[e][:, s, :].bitcast(FP8X4),
+                    rhs_scale=slot_scales[e][4 * s : P, :],
+                    start=False,
+                    stop=True,
+                )
 
         token_slots = []
         for r, pos in enumerate((pos1, pos2, pos3)):
@@ -217,16 +245,21 @@ def tile_moe_adp_relu2_kernel(
             nc.sync.dma_start(slots[:], pos)
             token_slots.append(slots)
 
-        w_raw = [load_rows(w[s * K_PASS : (s + 1) * K_PASS, :]) for s in range(PASSES)]
+        load_wb(E - 2)
         load_wb(E - 1)
+        w_raw = [load_rows(w[s * K_PASS : (s + 1) * K_PASS, :]) for s in range(PASSES)]
         gates = load([P, TOP, T], gate.rearrange("r p t -> p r t"))
 
         rectify(E - 1, "last_positive")
         square(E - 1, "last_h_grouped")
-        round_wb(E - 1)
         quantize_h(E - 1)
+        round_wb(E - 1, "V")
         quantize_wb(E - 1)
         second_layer(E - 1, "y_bank")
+        quantize_h(E - 2)
+        round_wb(E - 2, "S")
+        quantize_wb(E - 2)
+        second_layer(E - 2, "h_bank%d" % (PACK * E % H_BANKS))
 
         base_bank = psum.tile([P, T], F32, name="base_bank")
         for s in range(PASSES):
@@ -247,15 +280,18 @@ def tile_moe_adp_relu2_kernel(
                 stop=(s == PASSES - 1),
             )
 
-        terms = []
-        for r in range(TOP):
-            term = keep.tile([P, T], F32, name="term%d" % r)
-            nc.vector.tensor_tensor(term[:], slot_results[:].indirect(token_slots[r][:]), gates[:, r, :], MULT)
-            terms.append(term)
-        first = keep.tile([P, T], F32, name="first")
-        second = keep.tile([P, T], F32, name="second")
-        total = keep.tile([P, T], F32, name="total")
-        nc.vector.tensor_tensor(first[:], terms[0][:], terms[1][:], ADD)
-        nc.vector.tensor_tensor(second[:], terms[2][:], base_bank[:], ADD)
-        nc.vector.tensor_tensor(total[:], first[:], second[:], ADD)
-        nc.sync.dma_start(out=out, in_=total[:])
+        for part, (start, stop) in enumerate(((0, 384), (384, T))):
+            width = stop - start
+            terms = []
+            for r in range(TOP):
+                term = keep.tile([P, width], F32, name="term%d_%d" % (part, r))
+                offsets = token_slots[r][:, start // 16 : stop // 16]
+                nc.vector.tensor_tensor(term[:], slot_results[:].indirect(offsets), gates[:, r, start:stop], MULT)
+                terms.append(term)
+            first = keep.tile([P, width], F32, name="first%d" % part)
+            second = keep.tile([P, width], F32, name="second%d" % part)
+            total = keep.tile([P, width], F32, name="total%d" % part)
+            nc.vector.tensor_tensor(first[:], terms[0][:], terms[1][:], ADD)
+            nc.vector.tensor_tensor(second[:], terms[2][:], base_bank[:, start:stop], ADD)
+            nc.vector.tensor_tensor(total[:], first[:], second[:], ADD)
+            nc.sync.dma_start(out=out[:, start:stop], in_=total[:])

@@ -43,19 +43,18 @@ def tile_moe_adp_relu2_kernel(
         psum = ctx.enter_context(tc.psum_pool(name="psum", bufs=1))
 
         slot_tokens = keep.tile([P, SLOTS // 16], U16, name="slot_tokens")
-        nc.sync.dma_start(slot_tokens[:], offs)
 
         token_scales = keep.tile([P, T], U8, name="token_scales", align_bytes=64)
         nc.vector.memset(token_scales[:].bitcast(I32), 0)
 
-        token_words = [keep.tile([P, T], I32, name="token_words%d" % s, align_bytes=64) for s in range(PASSES)]
+        token_words = [keep.tile([P, T], I32, name="token_words%d" % s, align_bytes=256) for s in range(PASSES)]
         slot_results = keep.tile([P, SLOTS], F32, name="slot_results", align_bytes=64)
 
         loaded = []
 
         def load(shape, source):
             tag = "raw%d" % (len(loaded) % RAW_SLOTS)
-            raw = ring.tile(shape, F32, name=tag, align_bytes=64)
+            raw = ring.tile(shape, F32, name=tag, align_bytes=256)
             nc.sync.dma_start(out=raw[:], in_=source)
             loaded.append(tag)
             return raw
@@ -117,22 +116,14 @@ def tile_moe_adp_relu2_kernel(
             wb_mx[e] = quantize(wb_grouped[e], N, "wb%d" % (e % 3))
 
         def rectify(e, tag):
-            positive[e] = ring.tile([P, PACK, C], F32, name=tag, align_bytes=64)
+            positive[e] = ring.tile([P, PACK, C], F32, name=tag, align_bytes=256)
             for t in range(PACK):
-                if e == E - 1 and t % 2 == 1:
-                    nc.vector.tensor_scalar(positive[e][:, t, :], h_banks[e][t][:], 0.0, None, MAX)
-                else:
-                    nc.scalar.activation(out=positive[e][:, t, :], in_=h_banks[e][t][:], func=RELU)
+                nc.scalar.activation(out=positive[e][:, t, :], in_=h_banks[e][t][:], func=RELU)
 
         def square(e, tag):
             h_grouped[e] = ring.tile([P, PACK * C], BF16, name=tag, align_bytes=64)
             dst, src = interleaved(h_grouped[e], positive[e][:])
-            if e == E - 1:
-                half = C // 8
-                nc.scalar.activation(out=dst[:, :half], in_=src[:, :half], func=SQUARE)
-                nc.vector.tensor_tensor(dst[:, half:], src[:, half:], src[:, half:], MULT)
-            else:
-                nc.scalar.activation(out=dst, in_=src, func=SQUARE)
+            nc.scalar.activation(out=dst, in_=src, func=SQUARE)
 
         h_mx = {}
 
@@ -154,8 +145,10 @@ def tile_moe_adp_relu2_kernel(
             )
             nc.scalar.copy(out=slot_results[:, e * C : (e + 1) * C], in_=y_bank[:])
 
-        for s in range(PASSES):
-            load_words(s)
+        load_words(0)
+        nc.sync.dma_start(slot_tokens[:], offs)
+        load_words(1)
+        load_words(2)
         for q in range(4):
             nc.scalar.dma_start(
                 out=token_scales[32 * q : 32 * q + 4 * PASSES, :].bitcast(I32),
@@ -248,14 +241,35 @@ def tile_moe_adp_relu2_kernel(
         load_wb(E - 2)
         load_wb(E - 1)
         w_raw = [load_rows(w[s * K_PASS : (s + 1) * K_PASS, :]) for s in range(PASSES)]
-        gates = load([P, TOP, T], gate.rearrange("r p t -> p r t"))
+        gates = [load([P, T], gate[r]) for r in range(TOP)]
 
         rectify(E - 1, "last_positive")
-        square(E - 1, "last_h_grouped")
-        quantize_h(E - 1)
         round_wb(E - 1, "V")
         quantize_wb(E - 1)
-        second_layer(E - 1, "y_bank")
+        halves = []
+        for half, engine in enumerate("SV"):
+            grouped = ring.tile([P, PACK * P], BF16, name="half_grouped%d" % half, align_bytes=64)
+            dst, src = interleaved(grouped, positive[E - 1][:, :, half * P : (half + 1) * P])
+            if engine == "S":
+                nc.scalar.activation(out=dst, in_=src, func=SQUARE)
+            else:
+                nc.vector.tensor_tensor(dst, src, src, MULT)
+            halves.append(grouped)
+        wb_codes, wb_scales = wb_mx[E - 1]
+        for half in (1, 0):
+            h_codes, h_scales = quantize(halves[half], P, "half%d" % half)
+            y_bank = psum.tile([P, P], F32, name=("y_bank", "h_bank%d" % ((PACK * E + 1) % H_BANKS))[half])
+            nc.tensor.matmul_mx(
+                out=y_bank[:],
+                lhsT=wb_codes[:].bitcast(FP8X4),
+                lhsT_scale=wb_scales[:],
+                rhs=h_codes[:].bitcast(FP8X4),
+                rhs_scale=h_scales[:],
+                start=True,
+                stop=True,
+            )
+            first_slot = (E - 1) * C + half * P
+            nc.scalar.copy(out=slot_results[:, first_slot : first_slot + P], in_=y_bank[:])
         quantize_h(E - 2)
         round_wb(E - 2, "S")
         quantize_wb(E - 2)
@@ -265,10 +279,7 @@ def tile_moe_adp_relu2_kernel(
         for s in range(PASSES):
             w_grouped = keep.tile([P, PACK * N], BF16, name="w_grouped%d" % s, align_bytes=64)
             dst, src = interleaved(w_grouped, w_raw[s][:])
-            if s == 0:
-                nc.scalar.copy(out=dst, in_=src)
-            else:
-                nc.vector.tensor_copy(out=dst, in_=src)
+            round_to_bf16("VVS"[s], dst, src)
             w_codes, w_scales = quantize(w_grouped, N, "w%d" % s)
             nc.tensor.matmul_mx(
                 out=base_bank[:],
@@ -286,7 +297,7 @@ def tile_moe_adp_relu2_kernel(
             for r in range(TOP):
                 term = keep.tile([P, width], F32, name="term%d_%d" % (part, r))
                 offsets = token_slots[r][:, start // 16 : stop // 16]
-                nc.vector.tensor_tensor(term[:], slot_results[:].indirect(offsets), gates[:, r, start:stop], MULT)
+                nc.vector.tensor_tensor(term[:], slot_results[:].indirect(offsets), gates[r][:, start:stop], MULT)
                 terms.append(term)
             first = keep.tile([P, width], F32, name="first%d" % part)
             second = keep.tile([P, width], F32, name="second%d" % part)

@@ -23,14 +23,15 @@ ADD = mybir.AluOpType.add
 RELU = mybir.ActivationFunctionType.Relu
 SQUARE = mybir.ActivationFunctionType.Square
 
-CAST_ENGINES = ["SS", "SS", "SS", "SS", "SV", "SV"] + ["SS", "VV", "SV"] * 2 + ["SV", "VV", "SV"] * 2
-RAW_SLOTS = 14
-WORD_SLOTS = 6
-GATHER_AHEAD = 3
-GROUP_SLOTS = 4
-H_BANKS = 6
 CHUNKS = E * PASSES
-MAX = mybir.AluOpType.max
+SCALAR_SHARE = [64] * 4 + [32, 32] + [64, 0, 32] * 2 + [32, 0, 32] + [32, 0]
+LOAD_SIZES = [1] * 17
+RAW_SLOTS = 12
+GROUP_SLOTS = 4
+CODE_SLOTS = 4
+FREE_GATHERS = 3
+LATE_GATHERS = {0: 3, 2: 4, 4: 5}
+FIRST_TOKENS = 384
 
 
 def tile_moe_adp_relu2_kernel(
@@ -47,29 +48,22 @@ def tile_moe_adp_relu2_kernel(
         token_scales = keep.tile([P, T], U8, name="token_scales", align_bytes=64)
         nc.vector.memset(token_scales[:].bitcast(I32), 0)
 
-        token_words = [keep.tile([P, T], I32, name="token_words%d" % s, align_bytes=256) for s in range(PASSES)]
+        token_words = [keep.tile([P, T], I32, name="token_words%d" % s, align_bytes=256)[:] for s in range(PASSES)]
         slot_results = keep.tile([P, SLOTS], F32, name="slot_results", align_bytes=64)
 
-        loaded = []
-
-        def load(shape, source):
-            tag = "raw%d" % (len(loaded) % RAW_SLOTS)
-            raw = ring.tile(shape, F32, name=tag, align_bytes=256)
-            nc.sync.dma_start(out=raw[:], in_=source)
-            loaded.append(tag)
+        def load_rows(rows, tag):
+            raw = ring.tile([P, PACK, rows.shape[1]], F32, name=tag, align_bytes=256)
+            nc.sync.dma_start(out=raw[:], in_=rows.rearrange("(p j) c -> p j c", j=PACK))
             return raw
 
-        def load_rows(rows):
-            return load([P, PACK, rows.shape[1]], rows.rearrange("(p j) c -> p j c", j=PACK))
+        def load_passes(rows, tag):
+            count = rows.shape[0] // K_PASS
+            raw = ring.tile([P, count, PACK, rows.shape[1]], F32, name=tag, align_bytes=256)
+            nc.sync.dma_start(out=raw[:], in_=rows.rearrange("(a p j) c -> p a j c", p=P, j=PACK))
+            return [raw[:, a] for a in range(count)]
 
-        def load_words(s):
-            nc.sync.dma_start(
-                out=token_words[s][:],
-                in_=x_words[s].rearrange("p t d -> p (t d)").bitcast(I32),
-            )
-
-        def quantize(grouped, width, name, codes_tag=None):
-            codes = ring.tile([P, width], U32, name=codes_tag or name + "_codes", align_bytes=64)
+        def quantize(grouped, width, name):
+            codes = ring.tile([P, width], U32, name=name + "_codes", align_bytes=64)
             scales = ring.tile([P, width], U8, name=name + "_scales", align_bytes=64)
             nc.vector.quantize_mx(out=codes[:].bitcast(FP8X4), scales=scales[:], in_=grouped[:])
             return codes, scales
@@ -81,129 +75,138 @@ def tile_moe_adp_relu2_kernel(
                 nc.vector.tensor_copy(out=dst, in_=src)
 
         def interleaved(grouped, raw):
-            dst = grouped[:].rearrange("p (c i j) -> p c j i", i=4, j=PACK)
-            src = raw.rearrange("p j (c i) -> p c j i", i=4)
+            dst = grouped[:].rearrange("p (c i j) -> p c j i", i=2, j=PACK)
+            src = raw.rearrange("p j (c i) -> p c j i", i=2)
             return dst, src
+
+        def multiply(bank, weights, cols, moving_words, moving_scales, start, stop):
+            codes, scales = weights
+            nc.tensor.matmul_mx(
+                out=bank,
+                lhsT=codes[:, cols].bitcast(FP8X4),
+                lhsT_scale=scales[:, cols],
+                rhs=moving_words.bitcast(FP8X4),
+                rhs_scale=moving_scales,
+                start=start,
+                stop=stop,
+            )
+
+        def bank_tag(e, t):
+            return "bank%d" % (PACK * (e % 2) + t)
 
         slot_words = {}
         slot_scales = {}
 
-        def gather(e):
+        def gather(e, tag):
             offsets = slot_tokens[:, e * C // 16 : (e + 1) * C // 16]
-            slot_words[e] = ring.tile([P, PASSES, C], U32, name="last_grouped%d" % ((e + 1) % 4), align_bytes=64)
+            slot_words[e] = ring.tile([P, PASSES, C], U32, name=tag, align_bytes=64)
             for s in range(PASSES):
-                nc.vector.tensor_copy(slot_words[e][:, s, :], token_words[s][:].bitcast(U32).indirect(offsets))
-            slot_scales[e] = ring.tile([P, C], U8, name="h_grouped%d" % (e % 4), align_bytes=64)
+                nc.vector.tensor_copy(slot_words[e][:, s, :], token_words[s].bitcast(U32).indirect(offsets))
+            slot_scales[e] = ring.tile([P, C], U8, name="slot_scales%d" % e, align_bytes=64)
             nc.vector.tensor_copy(slot_scales[e][:], token_scales[:].indirect(offsets))
 
         h_banks = {}
         positive = {}
         h_grouped = {}
-        wb_mx = {}
-
+        h_mx = {}
         wb_raw = {}
         wb_grouped = {}
+        wb_mx = {}
 
         def load_wb(e):
-            wb_raw[e] = load_rows(wb[e])
+            raw = ring.tile([P, PACK, N], F32, name="wb_raw%d" % (e % 3), align_bytes=256)
+            rows = wb[e].rearrange("(m t r) n -> r m t n", t=PACK, r=2)
+            for r in range(2):
+                nc.sync.dma_start(out=raw[r:P:2], in_=rows[r])
+            wb_raw[e] = raw[:]
 
         def round_wb(e, engine):
             wb_grouped[e] = ring.tile([P, PACK * N], BF16, name="wb_grouped%d" % (e % 2), align_bytes=64)
-            dst, src = interleaved(wb_grouped[e], wb_raw[e][:])
+            dst, src = interleaved(wb_grouped[e], wb_raw[e])
             round_to_bf16(engine, dst, src)
 
         def quantize_wb(e):
             wb_mx[e] = quantize(wb_grouped[e], N, "wb%d" % (e % 3))
 
-        def rectify(e, tag):
+        def rectify(e, engines, tag):
             positive[e] = ring.tile([P, PACK, C], F32, name=tag, align_bytes=256)
-            for t in range(PACK):
-                nc.scalar.activation(out=positive[e][:, t, :], in_=h_banks[e][t][:], func=RELU)
+            for t, engine in enumerate(engines):
+                if engine == "S":
+                    nc.scalar.activation(out=positive[e][:, t, :], in_=h_banks[e][t][:], func=RELU)
+                else:
+                    nc.vector.tensor_scalar_max(positive[e][:, t, :], h_banks[e][t][:], 0.0)
 
-        def square(e, tag):
-            h_grouped[e] = ring.tile([P, PACK * C], BF16, name=tag, align_bytes=64)
+        def square(e):
+            h_grouped[e] = ring.tile([P, PACK * C], BF16, name="h_grouped%d" % (e % 2), align_bytes=64)
             dst, src = interleaved(h_grouped[e], positive[e][:])
             nc.scalar.activation(out=dst, in_=src, func=SQUARE)
-
-        h_mx = {}
 
         def quantize_h(e):
             h_mx[e] = quantize(h_grouped[e], C, "h%d" % (e % 3))
 
-        def second_layer(e, bank_tag):
+        def second_layer(e, tag):
             h_codes, h_scales = h_mx[e]
-            wb_codes, wb_scales = wb_mx[e]
-            y_bank = psum.tile([P, C], F32, name=bank_tag)
-            nc.tensor.matmul_mx(
-                out=y_bank[:],
-                lhsT=wb_codes[:].bitcast(FP8X4),
-                lhsT_scale=wb_scales[:],
-                rhs=h_codes[:].bitcast(FP8X4),
-                rhs_scale=h_scales[:],
-                start=True,
-                stop=True,
-            )
+            y_bank = psum.tile([P, C], F32, name=tag)
+            multiply(y_bank[:], wb_mx[e], slice(0, N), h_codes[:], h_scales[:], True, True)
             nc.scalar.copy(out=slot_results[:, e * C : (e + 1) * C], in_=y_bank[:])
 
-        load_words(0)
-        nc.sync.dma_start(slot_tokens[:], offs)
-        load_words(1)
-        load_words(2)
+        for s in range(PASSES):
+            nc.sync.dma_start(out=token_words[s], in_=x_words[s].rearrange("p t d -> p (t d)").bitcast(I32))
+            if s == 0:
+                nc.sync.dma_start(slot_tokens[:], offs)
         for q in range(4):
             nc.scalar.dma_start(
                 out=token_scales[32 * q : 32 * q + 4 * PASSES, :].bitcast(I32),
                 in_=x_scales[:, 4 * q : 4 * q + 4, :].bitcast(I32),
             )
-        gather(0)
-        gather(1)
+        for e in range(FREE_GATHERS):
+            gather(e, "slot_words%d" % e)
 
+        wa_rows = wa.rearrange("e k h -> (e k) h")
+        wa_raw = []
+        raw_tags = []
+        load_count = 0
         for chunk in range(CHUNKS - 1):
             e, s = divmod(chunk, PASSES)
-            wa_raw = load_rows(wa[e, s * K_PASS : (s + 1) * K_PASS, :])
-            raw_tag = loaded[-1]
-            if s == PASSES - 1:
-                grouped_tag = "last_grouped%d" % (e % 4)
+            if chunk == len(wa_raw):
+                size = LOAD_SIZES[load_count]
+                tag = "raw%d" % (load_count % RAW_SLOTS)
+                wa_raw.extend(load_passes(wa_rows[chunk * K_PASS : (chunk + size) * K_PASS, :], tag))
+                raw_tags.extend([tag] * size)
+                load_count = load_count + 1
+            if s == 0 and 0 < e < E - 1:
+                load_wb(e - 1)
+            if chunk in LATE_GATHERS:
+                grouped_tag = "slot_words%d" % LATE_GATHERS[chunk]
             else:
-                grouped_tag = "wa_grouped%d_%d" % (s, e % 2)
+                grouped_tag = "wa_grouped%d" % (chunk % GROUP_SLOTS)
             wa_grouped = ring.tile([P, PACK * H], BF16, name=grouped_tag, align_bytes=64)
-            dst = wa_grouped[:].rearrange("p (t m j) -> p m j t", t=PACK, j=PACK)
-            src = wa_raw[:].rearrange("p j (m t) -> p m j t", t=PACK)
-            for half, engine in enumerate(CAST_ENGINES[chunk]):
-                pair = slice(2 * half, 2 * half + 2)
-                if engine == "S":
-                    nc.scalar.copy(out=dst[:, :, :, pair], in_=src[:, :, :, pair])
-                else:
-                    nc.vector.tensor_copy(out=dst[:, :, :, pair], in_=src[:, :, :, pair])
-            if s == 0 and e + 2 < E:
-                gather(e + 2)
+            dst = wa_grouped[:].rearrange("p (t m r j) -> p m t j r", t=PACK, r=2, j=PACK)
+            src = wa_raw[chunk].rearrange("p j (m t r) -> p m t j r", t=PACK, r=2)
+            share = SCALAR_SHARE[chunk]
+            if share > 0:
+                round_to_bf16("S", dst[:, :share], src[:, :share])
+            if share < P // 2:
+                round_to_bf16("V", dst[:, share:], src[:, share:])
+            if s == 0 and e > 0:
+                behind_cast = SCALAR_SHARE[chunk] > 0
+                rectify(e - 1, "SSSS", raw_tags[chunk] if behind_cast else "positive%d" % (e % 2))
+                if e > 1:
+                    second_layer(e - 2, bank_tag(e - 1, 0))
+                square(e - 1)
             if s == 1 and 0 < e < E - 1:
                 round_wb(e - 1, "V")
-            if s == 2 and e > 0:
-                quantize_wb(e - 1)
                 quantize_h(e - 1)
-            wa_codes, wa_scales = quantize(wa_grouped, H, "wa%d" % (chunk % GROUP_SLOTS))
+                quantize_wb(e - 1)
+            wa_mx = quantize(wa_grouped, H, "wa%d" % (chunk % CODE_SLOTS))
+            if chunk in LATE_GATHERS:
+                gather(LATE_GATHERS[chunk], grouped_tag)
             if s == 0:
-                if e > 0:
-                    rectify(e - 1, raw_tag)
-                if e > 1:
-                    second_layer(e - 2, "h_bank%d" % (PACK * (e - 1) % H_BANKS))
-                if e > 0:
-                    square(e - 1, "h_grouped%d" % ((e - 1) % 4))
-                if 0 < e < E - 1:
-                    load_wb(e - 1)
-                h_banks[e] = [
-                    psum.tile([P, C], F32, name="h_bank%d" % ((PACK * e + t) % H_BANKS)) for t in range(PACK)
-                ]
+                h_banks[e] = [psum.tile([P, C], F32, name=bank_tag(e, t)) for t in range(PACK)]
             for t in range(PACK):
-                cols = slice(t * P, (t + 1) * P)
-                nc.tensor.matmul_mx(
-                    out=h_banks[e][t][:],
-                    lhsT=wa_codes[:, cols].bitcast(FP8X4),
-                    lhsT_scale=wa_scales[:, cols],
-                    rhs=slot_words[e][:, s, :].bitcast(FP8X4),
-                    rhs_scale=slot_scales[e][4 * s : P, :],
-                    start=(s == 0),
-                    stop=(s == PASSES - 1),
+                multiply(
+                    h_banks[e][t][:], wa_mx, slice(t * P, (t + 1) * P),
+                    slot_words[e][:, s, :], slot_scales[e][4 * s : P, :], s == 0, s == PASSES - 1,
                 )
 
         e, s = E - 1, PASSES - 1
@@ -211,39 +214,52 @@ def tile_moe_adp_relu2_kernel(
             ring.tile([P, 2 * H], BF16, name="pair_grouped%d" % pair, align_bytes=64) for pair in range(2)
         ]
         for half in range(2):
-            wa_raw = load_rows(wa[e, s * K_PASS : (s + 1) * K_PASS, half * H // 2 : (half + 1) * H // 2])
-            src = wa_raw[:].rearrange("p j (m t) -> p m j t", t=PACK)
+            last_raw = load_rows(
+                wa[e, s * K_PASS : (s + 1) * K_PASS, half * H // 2 : (half + 1) * H // 2], "last_raw%d" % half
+            )
+            src = last_raw[:].rearrange("p j (m t r) -> p m t j r", t=PACK, r=2)
             for pair, engine in enumerate("VS"):
-                dst = pair_grouped[pair][:].rearrange("p (t m j) -> p m j t", t=2, j=PACK)
+                dst = pair_grouped[pair][:].rearrange("p (t m r j) -> p m t j r", t=2, r=2, j=PACK)
                 round_to_bf16(
-                    engine, dst[:, half * P // 2 : (half + 1) * P // 2], src[:, :, :, 2 * pair : 2 * pair + 2]
+                    engine, dst[:, half * P // 4 : (half + 1) * P // 4], src[:, :, 2 * pair : 2 * pair + 2]
                 )
-        for pair in range(2):
-            wa_codes, wa_scales = quantize(pair_grouped[pair], 2 * P, "pair%d" % pair)
-            for t in range(2):
-                cols = slice(t * P, (t + 1) * P)
-                nc.tensor.matmul_mx(
-                    out=h_banks[e][2 * pair + t][:],
-                    lhsT=wa_codes[:, cols].bitcast(FP8X4),
-                    lhsT_scale=wa_scales[:, cols],
-                    rhs=slot_words[e][:, s, :].bitcast(FP8X4),
-                    rhs_scale=slot_scales[e][4 * s : P, :],
-                    start=False,
-                    stop=True,
-                )
+            if half == 0:
+                quantize_h(E - 2)
 
-        token_slots = []
-        for r, pos in enumerate((pos1, pos2, pos3)):
-            slots = keep.tile([P, T // 16], U16, name="token_slots%d" % r)
-            nc.sync.dma_start(slots[:], pos)
-            token_slots.append(slots)
-
+        gates = [keep.tile([P, T], F32, name="gate%d" % r) for r in range(TOP)]
+        token_slots = [keep.tile([P, T // 16], U16, name="token_slots%d" % r) for r in range(TOP)]
         load_wb(E - 2)
         load_wb(E - 1)
-        w_raw = [load_rows(w[s * K_PASS : (s + 1) * K_PASS, :]) for s in range(PASSES)]
-        gates = [load([P, T], gate[r]) for r in range(TOP)]
+        w_raw = [load_rows(w[s * K_PASS : (s + 1) * K_PASS, :], "w_raw%d" % s) for s in range(PASSES)]
+        for r, pos in enumerate((pos1, pos2, pos3)):
+            nc.sync.dma_start(token_slots[r][:], pos)
+        for r in range(TOP):
+            nc.sync.dma_start(out=gates[r][:], in_=gate[r])
 
-        rectify(E - 1, "last_positive")
+        s = PASSES - 1
+        for pair in range(2):
+            wa_mx = quantize(pair_grouped[pair], 2 * P, "pair%d" % pair)
+            for t in range(2):
+                multiply(
+                    h_banks[e][2 * pair + t][:], wa_mx, slice(t * P, (t + 1) * P),
+                    slot_words[e][:, s, :], slot_scales[e][4 * s : P, :], False, True,
+                )
+
+        def round_w(s, engine, tag):
+            grouped = ring.tile([P, PACK * N], BF16, name=tag, align_bytes=64)
+            dst, src = interleaved(grouped, w_raw[s][:])
+            round_to_bf16(engine, dst, src)
+            return grouped
+
+        def frozen_pass(s, grouped):
+            w_mx = quantize(grouped, N, "w%d" % s)
+            multiply(
+                base_bank[:], w_mx, slice(0, N), token_words[s], token_scales[4 * s : P, :],
+                s == 0, s == PASSES - 1,
+            )
+
+        round_wb(E - 2, "S")
+        rectify(E - 1, "SSSS", "positive0")
         round_wb(E - 1, "V")
         quantize_wb(E - 1)
         halves = []
@@ -255,54 +271,38 @@ def tile_moe_adp_relu2_kernel(
             else:
                 nc.vector.tensor_tensor(dst, src, src, MULT)
             halves.append(grouped)
-        wb_codes, wb_scales = wb_mx[E - 1]
+        quantize_wb(E - 2)
+        second_layer(E - 2, bank_tag(E - 2, 0))
         for half in (1, 0):
             h_codes, h_scales = quantize(halves[half], P, "half%d" % half)
-            y_bank = psum.tile([P, P], F32, name=("y_bank", "h_bank%d" % ((PACK * E + 1) % H_BANKS))[half])
-            nc.tensor.matmul_mx(
-                out=y_bank[:],
-                lhsT=wb_codes[:].bitcast(FP8X4),
-                lhsT_scale=wb_scales[:],
-                rhs=h_codes[:].bitcast(FP8X4),
-                rhs_scale=h_scales[:],
-                start=True,
-                stop=True,
-            )
+            y_bank = psum.tile([P, P], F32, name=bank_tag(E - 2, 1 + half))
+            multiply(y_bank[:], wb_mx[E - 1], slice(0, N), h_codes[:], h_scales[:], True, True)
             first_slot = (E - 1) * C + half * P
             nc.scalar.copy(out=slot_results[:, first_slot : first_slot + P], in_=y_bank[:])
-        quantize_h(E - 2)
-        round_wb(E - 2, "S")
-        quantize_wb(E - 2)
-        second_layer(E - 2, "h_bank%d" % (PACK * E % H_BANKS))
 
-        base_bank = psum.tile([P, T], F32, name="base_bank")
+        base_bank = psum.tile([P, T], F32, name=bank_tag(E - 2, 3))
+        w_tags = ["last_term%d" % r for r in range(TOP)]
         for s in range(PASSES):
-            w_grouped = keep.tile([P, PACK * N], BF16, name="w_grouped%d" % s, align_bytes=64)
-            dst, src = interleaved(w_grouped, w_raw[s][:])
-            round_to_bf16("VVS"[s], dst, src)
-            w_codes, w_scales = quantize(w_grouped, N, "w%d" % s)
-            nc.tensor.matmul_mx(
-                out=base_bank[:],
-                lhsT=w_codes[:].bitcast(FP8X4),
-                lhsT_scale=w_scales[:],
-                rhs=token_words[s][:].bitcast(FP8X4),
-                rhs_scale=token_scales[4 * s : P, :],
-                start=(s == 0),
-                stop=(s == PASSES - 1),
-            )
+            frozen_pass(s, round_w(s, "VVS"[s], "w_grouped%d" % s))
 
-        for part, (start, stop) in enumerate(((0, 384), (384, T))):
-            width = stop - start
-            terms = []
-            for r in range(TOP):
-                term = keep.tile([P, width], F32, name="term%d_%d" % (part, r))
-                offsets = token_slots[r][:, start // 16 : stop // 16]
-                nc.vector.tensor_tensor(term[:], slot_results[:].indirect(offsets), gates[r][:, start:stop], MULT)
-                terms.append(term)
-            first = keep.tile([P, width], F32, name="first%d" % part)
-            second = keep.tile([P, width], F32, name="second%d" % part)
-            total = keep.tile([P, width], F32, name="total%d" % part)
-            nc.vector.tensor_tensor(first[:], terms[0][:], terms[1][:], ADD)
-            nc.vector.tensor_tensor(second[:], terms[2][:], base_bank[:, start:stop], ADD)
-            nc.vector.tensor_tensor(total[:], first[:], second[:], ADD)
-            nc.sync.dma_start(out=out[:, start:stop], in_=total[:])
+        def weighted(r, start, stop, tag):
+            term = ring.tile([P, stop - start], F32, name=tag, align_bytes=64)
+            offsets = token_slots[r][:, start // 16 : stop // 16]
+            nc.vector.tensor_tensor(term[:], slot_results[:].indirect(offsets), gates[r][:, start:stop], MULT)
+            return term
+
+        def add(a, b, name):
+            total = keep.tile(list(a.shape), F32, name=name)
+            nc.vector.tensor_tensor(total[:], a, b, ADD)
+            return total
+
+        first_terms = [weighted(r, 0, FIRST_TOKENS, "first_term%d" % r) for r in range(TOP)]
+        first_sum = add(first_terms[0][:], first_terms[1][:], "first_pair")
+        first_base = add(first_terms[2][:], base_bank[:, 0:FIRST_TOKENS], "first_base")
+        last_terms = [weighted(r, FIRST_TOKENS, T, w_tags[r]) for r in range(TOP)]
+        first_sum = add(first_sum[:], first_base[:], "first_total")
+        nc.sync.dma_start(out=out[:, 0:FIRST_TOKENS], in_=first_sum[:])
+        last_pair = add(last_terms[0][:], last_terms[1][:], "last_pair")
+        last_base = add(last_terms[2][:], base_bank[:, FIRST_TOKENS:T], "last_base")
+        last_sum = add(last_pair[:], last_base[:], "last_total")
+        nc.sync.dma_start(out=out[:, FIRST_TOKENS:T], in_=last_sum[:])

@@ -24,13 +24,14 @@ RELU = mybir.ActivationFunctionType.Relu
 SQUARE = mybir.ActivationFunctionType.Square
 
 CHUNKS = E * PASSES
-SCALAR_SHARE = [64] * 4 + [32, 32] + [64, 0, 32] * 2 + [32, 0, 32] + [32, 0]
+SCALAR_SHARE = [64] * 4 + [48, 32] + [64, 0, 32] * 3 + [32, 0]
 LOAD_SIZES = [1] * 17
 RAW_SLOTS = 12
 GROUP_SLOTS = 4
 CODE_SLOTS = 4
-FREE_GATHERS = 3
-LATE_GATHERS = {0: 3, 2: 4, 4: 5}
+BATCH = SLOTS // 2
+WINDOW = 2 * T
+LATE_GATHERS = {0: 0, 2: 1, 4: 2}
 FIRST_TOKENS = 384
 
 
@@ -45,10 +46,13 @@ def tile_moe_adp_relu2_kernel(
 
         slot_tokens = keep.tile([P, SLOTS // 16], U16, name="slot_tokens")
 
-        token_scales = keep.tile([P, T], U8, name="token_scales", align_bytes=64)
+        token_scales = keep.tile([P, WINDOW], U8, name="token_scales", align_bytes=64)
         nc.vector.memset(token_scales[:].bitcast(I32), 0)
 
-        token_words = [keep.tile([P, T], I32, name="token_words%d" % s, align_bytes=256)[:] for s in range(PASSES)]
+        windows = [keep.tile([P, WINDOW], I32, name="token_words%d" % s, align_bytes=256) for s in range(PASSES)]
+        for window in windows:
+            nc.vector.memset(window[:, T:], 0)
+        token_words = [window[:, :T] for window in windows]
         slot_results = keep.tile([P, SLOTS], F32, name="slot_results", align_bytes=64)
 
         def load_rows(rows, tag):
@@ -97,13 +101,20 @@ def tile_moe_adp_relu2_kernel(
         slot_words = {}
         slot_scales = {}
 
-        def gather(e, tag):
-            offsets = slot_tokens[:, e * C // 16 : (e + 1) * C // 16]
-            slot_words[e] = ring.tile([P, PASSES, C], U32, name=tag, align_bytes=64)
-            for s in range(PASSES):
-                nc.vector.tensor_copy(slot_words[e][:, s, :], token_words[s].bitcast(U32).indirect(offsets))
-            slot_scales[e] = ring.tile([P, C], U8, name="slot_scales%d" % e, align_bytes=64)
-            nc.vector.tensor_copy(slot_scales[e][:], token_scales[:].indirect(offsets))
+        def batch_offsets(batch):
+            return slot_tokens[:, batch * BATCH // 16 : (batch + 1) * BATCH // 16]
+
+        def gather_words(batch, s, tag):
+            words = ring.tile([P, BATCH], U32, name=tag, align_bytes=64)
+            nc.vector.tensor_copy(words[:], windows[s][:].bitcast(U32).indirect(batch_offsets(batch)))
+            for i in range(BATCH // C):
+                slot_words[batch * BATCH // C + i, s] = words[:, i * C : (i + 1) * C]
+
+        def gather_scales(batch, tag):
+            scales = ring.tile([P, BATCH], U8, name=tag, align_bytes=64)
+            nc.vector.tensor_copy(scales[:], token_scales[:].indirect(batch_offsets(batch)))
+            for i in range(BATCH // C):
+                slot_scales[batch * BATCH // C + i] = scales[:, i * C : (i + 1) * C]
 
         h_banks = {}
         positive = {}
@@ -156,11 +167,13 @@ def tile_moe_adp_relu2_kernel(
                 nc.sync.dma_start(slot_tokens[:], offs)
         for q in range(4):
             nc.scalar.dma_start(
-                out=token_scales[32 * q : 32 * q + 4 * PASSES, :].bitcast(I32),
+                out=token_scales[32 * q : 32 * q + 4 * PASSES, :T].bitcast(I32),
                 in_=x_scales[:, 4 * q : 4 * q + 4, :].bitcast(I32),
             )
-        for e in range(FREE_GATHERS):
-            gather(e, "slot_words%d" % e)
+        for s in range(PASSES):
+            gather_words(0, s, "early_words%d" % s)
+        gather_scales(0, "early_scales")
+        gather_scales(1, "late_scales")
 
         wa_rows = wa.rearrange("e k h -> (e k) h")
         wa_raw = []
@@ -177,7 +190,7 @@ def tile_moe_adp_relu2_kernel(
             if s == 0 and 0 < e < E - 1:
                 load_wb(e - 1)
             if chunk in LATE_GATHERS:
-                grouped_tag = "slot_words%d" % LATE_GATHERS[chunk]
+                grouped_tag = "late_words%d" % LATE_GATHERS[chunk]
             else:
                 grouped_tag = "wa_grouped%d" % (chunk % GROUP_SLOTS)
             wa_grouped = ring.tile([P, PACK * H], BF16, name=grouped_tag, align_bytes=64)
@@ -200,13 +213,13 @@ def tile_moe_adp_relu2_kernel(
                 quantize_wb(e - 1)
             wa_mx = quantize(wa_grouped, H, "wa%d" % (chunk % CODE_SLOTS))
             if chunk in LATE_GATHERS:
-                gather(LATE_GATHERS[chunk], grouped_tag)
+                gather_words(1, LATE_GATHERS[chunk], grouped_tag)
             if s == 0:
                 h_banks[e] = [psum.tile([P, C], F32, name=bank_tag(e, t)) for t in range(PACK)]
             for t in range(PACK):
                 multiply(
                     h_banks[e][t][:], wa_mx, slice(t * P, (t + 1) * P),
-                    slot_words[e][:, s, :], slot_scales[e][4 * s : P, :], s == 0, s == PASSES - 1,
+                    slot_words[e, s], slot_scales[e][4 * s : P, :], s == 0, s == PASSES - 1,
                 )
 
         e, s = E - 1, PASSES - 1
@@ -242,7 +255,7 @@ def tile_moe_adp_relu2_kernel(
             for t in range(2):
                 multiply(
                     h_banks[e][2 * pair + t][:], wa_mx, slice(t * P, (t + 1) * P),
-                    slot_words[e][:, s, :], slot_scales[e][4 * s : P, :], False, True,
+                    slot_words[e, s], slot_scales[e][4 * s : P, :], False, True,
                 )
 
         def round_w(s, engine, tag):
@@ -254,7 +267,7 @@ def tile_moe_adp_relu2_kernel(
         def frozen_pass(s, grouped):
             w_mx = quantize(grouped, N, "w%d" % s)
             multiply(
-                base_bank[:], w_mx, slice(0, N), token_words[s], token_scales[4 * s : P, :],
+                base_bank[:], w_mx, slice(0, N), token_words[s], token_scales[4 * s : P, :T],
                 s == 0, s == PASSES - 1,
             )
 
@@ -292,15 +305,15 @@ def tile_moe_adp_relu2_kernel(
             return term
 
         def add(a, b, name):
-            total = keep.tile(list(a.shape), F32, name=name)
+            total = ring.tile(list(a.shape), F32, name=name, align_bytes=64)
             nc.vector.tensor_tensor(total[:], a, b, ADD)
             return total
 
-        first_terms = [weighted(r, 0, FIRST_TOKENS, "first_term%d" % r) for r in range(TOP)]
-        first_sum = add(first_terms[0][:], first_terms[1][:], "first_pair")
-        first_base = add(first_terms[2][:], base_bank[:, 0:FIRST_TOKENS], "first_base")
+        first_terms = [weighted(r, 0, FIRST_TOKENS, "wa_grouped%d" % r) for r in range(TOP)]
+        first_sum = add(first_terms[0][:], first_terms[1][:], "early_words0")
+        first_base = add(first_terms[2][:], base_bank[:, 0:FIRST_TOKENS], "early_words1")
         last_terms = [weighted(r, FIRST_TOKENS, T, w_tags[r]) for r in range(TOP)]
-        first_sum = add(first_sum[:], first_base[:], "first_total")
+        first_sum = add(first_sum[:], first_base[:], "early_words2")
         nc.sync.dma_start(out=out[:, 0:FIRST_TOKENS], in_=first_sum[:])
         last_pair = add(last_terms[0][:], last_terms[1][:], "last_pair")
         last_base = add(last_terms[2][:], base_bank[:, FIRST_TOKENS:T], "last_base")

@@ -24,7 +24,7 @@ RELU = mybir.ActivationFunctionType.Relu
 SQUARE = mybir.ActivationFunctionType.Square
 
 CHUNKS = E * PASSES
-SCALAR_SHARE = [64] * 4 + [48, 32] + [64, 0, 32] * 3 + [32, 0]
+SCALAR_SHARE = [64] * 5 + [32] + [64, 0, 32] * 3 + [32, 0]
 LOAD_SIZES = [1] * 17
 RAW_SLOTS = 12
 GROUP_SLOTS = 4
@@ -201,7 +201,7 @@ def tile_moe_adp_relu2_kernel(
                 round_to_bf16("S", dst[:, :share], src[:, :share])
             if share < P // 2:
                 round_to_bf16("V", dst[:, share:], src[:, share:])
-            if s == 0 and e > 0:
+            if e > 0 and s == (1 if e == 1 else 0):
                 behind_cast = SCALAR_SHARE[chunk] > 0
                 rectify(e - 1, "SSSS", raw_tags[chunk] if behind_cast else "positive%d" % (e % 2))
                 if e > 1:

@@ -236,8 +236,6 @@ def tile_moe_adp_relu2_kernel(
                 round_to_bf16(
                     engine, dst[:, half * P // 4 : (half + 1) * P // 4], src[:, :, 2 * pair : 2 * pair + 2]
                 )
-            if half == 0:
-                quantize_h(E - 2)
 
         gates = [keep.tile([P, T], F32, name="gate%d" % r) for r in range(TOP)]
         token_slots = [keep.tile([P, T // 16], U16, name="token_slots%d" % r) for r in range(TOP)]
@@ -257,6 +255,11 @@ def tile_moe_adp_relu2_kernel(
                     h_banks[e][2 * pair + t][:], wa_mx, slice(t * P, (t + 1) * P),
                     slot_words[e, s], slot_scales[e][4 * s : P, :], False, True,
                 )
+
+        h_codes = ring.tile([P, C], U32, name="pair_grouped0", align_bytes=64)
+        h_scales = ring.tile([P, C], U8, name="late_h_scales", align_bytes=64)
+        nc.vector.quantize_mx(out=h_codes[:].bitcast(FP8X4), scales=h_scales[:], in_=h_grouped[E - 2][:])
+        h_mx[E - 2] = (h_codes, h_scales)
 
         def round_w(s, engine, tag):
             grouped = ring.tile([P, PACK * N], BF16, name=tag, align_bytes=64)

@@ -24,14 +24,13 @@ RELU = mybir.ActivationFunctionType.Relu
 SQUARE = mybir.ActivationFunctionType.Square
 
 CHUNKS = E * PASSES
-SCALAR_SHARE = [64] * 5 + [32] + [64, 0, 32] * 3 + [32, 0]
+SCALAR_SHARE = [64] * 5 + [48] + [64, 0, 32] * 3 + [32, 0]
 LOAD_SIZES = [1] * 17
 RAW_SLOTS = 12
 GROUP_SLOTS = 4
 CODE_SLOTS = 4
-BATCH = SLOTS // 2
-WINDOW = 2 * T
-LATE_GATHERS = {0: 0, 2: 1, 4: 2}
+FREE_GATHERS = 3
+LATE_GATHERS = {0: 3, 2: 4, 4: 5}
 FIRST_TOKENS = 384
 
 
@@ -46,13 +45,10 @@ def tile_moe_adp_relu2_kernel(
 
         slot_tokens = keep.tile([P, SLOTS // 16], U16, name="slot_tokens")
 
-        token_scales = keep.tile([P, WINDOW], U8, name="token_scales", align_bytes=64)
+        token_scales = keep.tile([P, T], U8, name="token_scales", align_bytes=64)
         nc.vector.memset(token_scales[:].bitcast(I32), 0)
 
-        windows = [keep.tile([P, WINDOW], I32, name="token_words%d" % s, align_bytes=256) for s in range(PASSES)]
-        for window in windows:
-            nc.vector.memset(window[:, T:], 0)
-        token_words = [window[:, :T] for window in windows]
+        token_words = [keep.tile([P, T], I32, name="token_words%d" % s, align_bytes=256)[:] for s in range(PASSES)]
         slot_results = keep.tile([P, SLOTS], F32, name="slot_results", align_bytes=64)
 
         def load_rows(rows, tag):
@@ -101,20 +97,13 @@ def tile_moe_adp_relu2_kernel(
         slot_words = {}
         slot_scales = {}
 
-        def batch_offsets(batch):
-            return slot_tokens[:, batch * BATCH // 16 : (batch + 1) * BATCH // 16]
-
-        def gather_words(batch, s, tag):
-            words = ring.tile([P, BATCH], U32, name=tag, align_bytes=64)
-            nc.vector.tensor_copy(words[:], windows[s][:].bitcast(U32).indirect(batch_offsets(batch)))
-            for i in range(BATCH // C):
-                slot_words[batch * BATCH // C + i, s] = words[:, i * C : (i + 1) * C]
-
-        def gather_scales(batch, tag):
-            scales = ring.tile([P, BATCH], U8, name=tag, align_bytes=64)
-            nc.vector.tensor_copy(scales[:], token_scales[:].indirect(batch_offsets(batch)))
-            for i in range(BATCH // C):
-                slot_scales[batch * BATCH // C + i] = scales[:, i * C : (i + 1) * C]
+        def gather(e, tag):
+            offsets = slot_tokens[:, e * C // 16 : (e + 1) * C // 16]
+            slot_words[e] = ring.tile([P, PASSES, C], U32, name=tag, align_bytes=64)
+            for s in range(PASSES):
+                nc.vector.tensor_copy(slot_words[e][:, s, :], token_words[s].bitcast(U32).indirect(offsets))
+            slot_scales[e] = ring.tile([P, C], U8, name="slot_scales%d" % e, align_bytes=64)
+            nc.vector.tensor_copy(slot_scales[e][:], token_scales[:].indirect(offsets))
 
         h_banks = {}
         positive = {}
@@ -167,13 +156,11 @@ def tile_moe_adp_relu2_kernel(
                 nc.sync.dma_start(slot_tokens[:], offs)
         for q in range(4):
             nc.scalar.dma_start(
-                out=token_scales[32 * q : 32 * q + 4 * PASSES, :T].bitcast(I32),
+                out=token_scales[32 * q : 32 * q + 4 * PASSES, :].bitcast(I32),
                 in_=x_scales[:, 4 * q : 4 * q + 4, :].bitcast(I32),
             )
-        for s in range(PASSES):
-            gather_words(0, s, "early_words%d" % s)
-        gather_scales(0, "early_scales")
-        gather_scales(1, "late_scales")
+        for e in range(FREE_GATHERS):
+            gather(e, "slot_words%d" % e)
 
         wa_rows = wa.rearrange("e k h -> (e k) h")
         wa_raw = []
@@ -190,7 +177,7 @@ def tile_moe_adp_relu2_kernel(
             if s == 0 and 0 < e < E - 1:
                 load_wb(e - 1)
             if chunk in LATE_GATHERS:
-                grouped_tag = "late_words%d" % LATE_GATHERS[chunk]
+                grouped_tag = "slot_words%d" % LATE_GATHERS[chunk]
             else:
                 grouped_tag = "wa_grouped%d" % (chunk % GROUP_SLOTS)
             wa_grouped = ring.tile([P, PACK * H], BF16, name=grouped_tag, align_bytes=64)
@@ -213,13 +200,13 @@ def tile_moe_adp_relu2_kernel(
                 quantize_wb(e - 1)
             wa_mx = quantize(wa_grouped, H, "wa%d" % (chunk % CODE_SLOTS))
             if chunk in LATE_GATHERS:
-                gather_words(1, LATE_GATHERS[chunk], grouped_tag)
+                gather(LATE_GATHERS[chunk], grouped_tag)
             if s == 0:
                 h_banks[e] = [psum.tile([P, C], F32, name=bank_tag(e, t)) for t in range(PACK)]
             for t in range(PACK):
                 multiply(
                     h_banks[e][t][:], wa_mx, slice(t * P, (t + 1) * P),
-                    slot_words[e, s], slot_scales[e][4 * s : P, :], s == 0, s == PASSES - 1,
+                    slot_words[e][:, s, :], slot_scales[e][4 * s : P, :], s == 0, s == PASSES - 1,
                 )
 
         e, s = E - 1, PASSES - 1
@@ -253,7 +240,7 @@ def tile_moe_adp_relu2_kernel(
             for t in range(2):
                 multiply(
                     h_banks[e][2 * pair + t][:], wa_mx, slice(t * P, (t + 1) * P),
-                    slot_words[e, s], slot_scales[e][4 * s : P, :], False, True,
+                    slot_words[e][:, s, :], slot_scales[e][4 * s : P, :], False, True,
                 )
 
         h_codes = ring.tile([P, C], U32, name="pair_grouped0", align_bytes=64)
@@ -270,7 +257,7 @@ def tile_moe_adp_relu2_kernel(
         def frozen_pass(s, grouped):
             w_mx = quantize(grouped, N, "w%d" % s)
             multiply(
-                base_bank[:], w_mx, slice(0, N), token_words[s], token_scales[4 * s : P, :T],
+                base_bank[:], w_mx, slice(0, N), token_words[s], token_scales[4 * s : P, :],
                 s == 0, s == PASSES - 1,
             )
 
@@ -313,10 +300,10 @@ def tile_moe_adp_relu2_kernel(
             return total
 
         first_terms = [weighted(r, 0, FIRST_TOKENS, "wa_grouped%d" % r) for r in range(TOP)]
-        first_sum = add(first_terms[0][:], first_terms[1][:], "early_words0")
-        first_base = add(first_terms[2][:], base_bank[:, 0:FIRST_TOKENS], "early_words1")
+        first_sum = add(first_terms[0][:], first_terms[1][:], "slot_words0")
+        first_base = add(first_terms[2][:], base_bank[:, 0:FIRST_TOKENS], "slot_words1")
         last_terms = [weighted(r, FIRST_TOKENS, T, w_tags[r]) for r in range(TOP)]
-        first_sum = add(first_sum[:], first_base[:], "early_words2")
+        first_sum = add(first_sum[:], first_base[:], "slot_words2")
         nc.sync.dma_start(out=out[:, 0:FIRST_TOKENS], in_=first_sum[:])
         last_pair = add(last_terms[0][:], last_terms[1][:], "last_pair")
         last_base = add(last_terms[2][:], base_bank[:, FIRST_TOKENS:T], "last_base")

@@ -24,14 +24,15 @@ RELU = mybir.ActivationFunctionType.Relu
 SQUARE = mybir.ActivationFunctionType.Square
 
 CHUNKS = E * PASSES
-SCALAR_SHARE = [64] * 5 + [48] + [64, 0, 32] * 3 + [32, 0]
+SCALAR_SHARE = [64] * 3 + [64, 0, 36] * 4 + [0, 0]
 LOAD_SIZES = [1] * 17
-RAW_SLOTS = 12
+RAW_SLOTS = 11
 GROUP_SLOTS = 4
 CODE_SLOTS = 4
 FREE_GATHERS = 3
-LATE_GATHERS = {0: 3, 2: 4, 4: 5}
+LATE_GATHERS = {5: 3, 8: 4, 11: 5}
 FIRST_TOKENS = 384
+EARLY = 4
 
 
 def tile_moe_adp_relu2_kernel(
@@ -112,13 +113,10 @@ def tile_moe_adp_relu2_kernel(
         wb_raw = {}
         wb_grouped = {}
         wb_mx = {}
+        early_pairs = []
 
         def load_wb(e):
-            raw = ring.tile([P, PACK, N], F32, name="wb_raw%d" % (e % 3), align_bytes=256)
-            rows = wb[e].rearrange("(m t r) n -> r m t n", t=PACK, r=2)
-            for r in range(2):
-                nc.sync.dma_start(out=raw[r:P:2], in_=rows[r])
-            wb_raw[e] = raw[:]
+            wb_raw[e] = load_rows(wb[e], "wb_raw%d" % e)[:]
 
         def round_wb(e, engine):
             wb_grouped[e] = ring.tile([P, PACK * N], BF16, name="wb_grouped%d" % (e % 2), align_bytes=64)
@@ -142,13 +140,21 @@ def tile_moe_adp_relu2_kernel(
             nc.scalar.activation(out=dst, in_=src, func=SQUARE)
 
         def quantize_h(e):
-            h_mx[e] = quantize(h_grouped[e], C, "h%d" % (e % 3))
+            h_mx[e] = quantize(h_grouped[e], C, "h%d" % e)
 
         def second_layer(e, tag):
             h_codes, h_scales = h_mx[e]
             y_bank = psum.tile([P, C], F32, name=tag)
             multiply(y_bank[:], wb_mx[e], slice(0, N), h_codes[:], h_scales[:], True, True)
             nc.scalar.copy(out=slot_results[:, e * C : (e + 1) * C], in_=y_bank[:])
+
+        def early_layer(adapters, tag, engine):
+            y_bank = psum.tile([P, len(adapters), C], F32, name=tag)
+            for a, e in enumerate(adapters):
+                h_codes, h_scales = h_mx[e]
+                multiply(y_bank[:, a, :], wb_mx["early%d" % (e // 2)], slice(a * N, (a + 1) * N), h_codes[:], h_scales[:], True, True)
+            cols = slice(adapters[0] * C, (adapters[-1] + 1) * C)
+            round_to_bf16(engine, slot_results[:, cols], y_bank[:].rearrange("p a c -> p (a c)"))
 
         for s in range(PASSES):
             nc.sync.dma_start(out=token_words[s], in_=x_words[s].rearrange("p t d -> p (t d)").bitcast(I32))
@@ -174,31 +180,47 @@ def tile_moe_adp_relu2_kernel(
                 wa_raw.extend(load_passes(wa_rows[chunk * K_PASS : (chunk + size) * K_PASS, :], tag))
                 raw_tags.extend([tag] * size)
                 load_count = load_count + 1
-            if s == 0 and 0 < e < E - 1:
-                load_wb(e - 1)
+            if (e, s) == (EARLY, PASSES - 1):
+                early_raw = ring.tile([P, EARLY, PACK, N], F32, name="early_raw", align_bytes=256)
+                nc.sync.dma_start(out=early_raw[:], in_=wb[0:EARLY].rearrange("e (p j) n -> p e j n", j=PACK))
             if chunk in LATE_GATHERS:
                 grouped_tag = "slot_words%d" % LATE_GATHERS[chunk]
             else:
                 grouped_tag = "wa_grouped%d" % (chunk % GROUP_SLOTS)
             wa_grouped = ring.tile([P, PACK * H], BF16, name=grouped_tag, align_bytes=64)
-            dst = wa_grouped[:].rearrange("p (t m r j) -> p m t j r", t=PACK, r=2, j=PACK)
-            src = wa_raw[chunk].rearrange("p j (m t r) -> p m t j r", t=PACK, r=2)
-            share = SCALAR_SHARE[chunk]
-            if share > 0:
-                round_to_bf16("S", dst[:, :share], src[:, :share])
-            if share < P // 2:
-                round_to_bf16("V", dst[:, share:], src[:, share:])
-            if e > 0 and s == (1 if e == 1 else 0):
+            if e < E - 1:
+                dst = wa_grouped[:].rearrange("p (u v m j) -> p u m j v", u=2, v=2, j=PACK)
+                src = wa_raw[chunk].rearrange("p j (m u v) -> p u m j v", u=2, v=2)
+                share = 2 * SCALAR_SHARE[chunk]
+                if share > 0:
+                    round_to_bf16("S", dst[:, :, :share], src[:, :, :share])
+                if share < P:
+                    round_to_bf16("V", dst[:, :, share:], src[:, :, share:])
+            else:
+                dst = wa_grouped[:].rearrange("p (t m r j) -> p m t j r", t=PACK, r=2, j=PACK)
+                src = wa_raw[chunk].rearrange("p j (m t r) -> p m t j r", t=PACK, r=2)
+                round_to_bf16("V", dst, src)
+            if e > 0 and s == 0:
                 behind_cast = SCALAR_SHARE[chunk] > 0
-                rectify(e - 1, "SSSS", raw_tags[chunk] if behind_cast else "positive%d" % (e % 2))
-                if e > 1:
-                    second_layer(e - 2, bank_tag(e - 1, 0))
+                rectify(e - 1, "SSSS", raw_tags[chunk] if behind_cast else "early_raw")
                 square(e - 1)
-            if s == 1 and 0 < e < E - 1:
-                round_wb(e - 1, "V")
-                quantize_h(e - 1)
-                quantize_wb(e - 1)
+            if (e, s) == (EARLY + 1, 0):
+                early_layer([0, 1], bank_tag(e, 2), "S")
+                early_layer([2, 3], bank_tag(e, 3), "S")
             wa_mx = quantize(wa_grouped, H, "wa%d" % (chunk % CODE_SLOTS))
+            if s == 1 and 0 < e < E - 1:
+                quantize_h(e - 1)
+            if (e, s) == (EARLY, PASSES - 1):
+                for pair, (engine, tag) in enumerate((("S", "early_grouped"), ("V", grouped_tag))):
+                    grouped = ring.tile([P, 2 * PACK * N], BF16, name=tag, align_bytes=64)
+                    round_to_bf16(
+                        engine,
+                        grouped[:].rearrange("p (e c i j) -> p e c j i", e=2, i=2, j=PACK),
+                        early_raw[:, 2 * pair : 2 * pair + 2].rearrange("p e j (c i) -> p e c j i", i=2),
+                    )
+                    early_pairs.append(grouped)
+                for pair in (1, 0):
+                    wb_mx["early%d" % pair] = quantize(early_pairs[pair], 2 * N, "early%d" % pair)
             if chunk in LATE_GATHERS:
                 gather(LATE_GATHERS[chunk], grouped_tag)
             if s == 0:
@@ -227,7 +249,11 @@ def tile_moe_adp_relu2_kernel(
         gates = [keep.tile([P, T], F32, name="gate%d" % r) for r in range(TOP)]
         token_slots = [keep.tile([P, T // 16], U16, name="token_slots%d" % r) for r in range(TOP)]
         load_wb(E - 2)
-        load_wb(E - 1)
+        last_wb = ring.tile([P, PACK, N], F32, name="wb_raw5", align_bytes=256)
+        rows = wb[E - 1].rearrange("(m t r) n -> r m t n", t=PACK, r=2)
+        for r in range(2):
+            nc.sync.dma_start(out=last_wb[r:P:2], in_=rows[r])
+        wb_raw[E - 1] = last_wb[:]
         w_raw = [load_rows(w[s * K_PASS : (s + 1) * K_PASS, :], "w_raw%d" % s) for s in range(PASSES)]
         for r, pos in enumerate((pos1, pos2, pos3)):
             nc.sync.dma_start(token_slots[r][:], pos)

@@ -8,6 +8,7 @@ PACK = 4
 K_PASS = P * PACK
 PASSES = K // K_PASS
 SLOTS = E * C
+CHUNKS = E * PASSES
 
 FLOPS = 2 * K * N * T + 2 * SLOTS * K * H + 2 * SLOTS * H * N
 
@@ -22,17 +23,19 @@ MULT = mybir.AluOpType.mult
 ADD = mybir.AluOpType.add
 RELU = mybir.ActivationFunctionType.Relu
 SQUARE = mybir.ActivationFunctionType.Square
+COPY = mybir.ActivationFunctionType.Copy
 
-CHUNKS = E * PASSES
-SCALAR_SHARE = [64] * 3 + [64, 0, 36] * 4 + [0, 0]
-LOAD_SIZES = [1] * 17
-RAW_SLOTS = 11
+RAW_SLOTS = 12
 GROUP_SLOTS = 4
-CODE_SLOTS = 4
-FREE_GATHERS = 3
-LATE_GATHERS = {5: 3, 8: 4, 11: 5}
-FIRST_TOKENS = 384
+CODE_SLOTS = 6
+HEAD_ADAPTERS = 3
 EARLY = 4
+HALF = C // 2
+SCALAR_SHARE = [128] * 4 + [88, 0] + [128, 0, 68] * 2 + [128, 0, 30] + [0, 44]
+RELU_BEHIND = (4, 6, 9, 12)
+SPLIT_17B = 88
+FIRST_TOKENS = 256
+LATE_BYTES = PACK * H * 2
 
 
 def tile_moe_adp_relu2_kernel(
@@ -42,43 +45,44 @@ def tile_moe_adp_relu2_kernel(
     with ExitStack() as ctx:
         keep = ctx.enter_context(tc.tile_pool(name="keep", bufs=1))
         ring = ctx.enter_context(tc.tile_pool(name="ring", bufs=1))
+        late = ctx.enter_context(tc.tile_pool(name="late", bufs=1))
         psum = ctx.enter_context(tc.psum_pool(name="psum", bufs=1))
 
         slot_tokens = keep.tile([P, SLOTS // 16], U16, name="slot_tokens")
-
+        token_slots = [keep.tile([P, T // 16], U16, name="token_slots%d" % r) for r in range(TOP)]
         token_scales = keep.tile([P, T], U8, name="token_scales", align_bytes=64)
-        nc.vector.memset(token_scales[:].bitcast(I32), 0)
-
-        token_words = [keep.tile([P, T], I32, name="token_words%d" % s, align_bytes=256)[:] for s in range(PASSES)]
+        token_words = [keep.tile([P, T], I32, name="token_words%d" % s, align_bytes=256) for s in range(PASSES)]
         slot_results = keep.tile([P, SLOTS], F32, name="slot_results", align_bytes=64)
+        nc.gpsimd.memset(token_scales[:].bitcast(I32), 0)
 
-        def load_rows(rows, tag):
-            raw = ring.tile([P, PACK, rows.shape[1]], F32, name=tag, align_bytes=256)
-            nc.sync.dma_start(out=raw[:], in_=rows.rearrange("(p j) c -> p j c", j=PACK))
-            return raw
-
-        def load_passes(rows, tag):
-            count = rows.shape[0] // K_PASS
-            raw = ring.tile([P, count, PACK, rows.shape[1]], F32, name=tag, align_bytes=256)
-            nc.sync.dma_start(out=raw[:], in_=rows.rearrange("(a p j) c -> p a j c", p=P, j=PACK))
-            return [raw[:, a] for a in range(count)]
-
-        def quantize(grouped, width, name):
-            codes = ring.tile([P, width], U32, name=name + "_codes", align_bytes=64)
-            scales = ring.tile([P, width], U8, name=name + "_scales", align_bytes=64)
-            nc.vector.quantize_mx(out=codes[:].bitcast(FP8X4), scales=scales[:], in_=grouped[:])
-            return codes, scales
-
-        def round_to_bf16(engine, dst, src):
+        def move(engine, dst, src):
             if engine == "S":
                 nc.scalar.copy(out=dst, in_=src)
             else:
                 nc.vector.tensor_copy(out=dst, in_=src)
 
-        def interleaved(grouped, raw):
-            dst = grouped[:].rearrange("p (c i j) -> p c j i", i=2, j=PACK)
+        def raw_tile(shape, slot):
+            return ring.tile(shape, F32, name="raw%d" % (slot % RAW_SLOTS), align_bytes=256)
+
+        def load_rows(rows, slot):
+            raw = raw_tile([P, PACK, rows.shape[1]], slot)
+            nc.sync.dma_start(out=raw[:], in_=rows.rearrange("(p j) c -> p j c", j=PACK))
+            return raw
+
+        def mx_tiles(width, name, codes_tag=None):
+            codes = ring.tile([P, width], U32, name=codes_tag or name + "_codes", align_bytes=64)
+            scales = ring.tile([P, width], U8, name=name + "_scales", align_bytes=64)
+            return codes, scales
+
+        def quantize(grouped, width, name, codes_tag=None):
+            codes, scales = mx_tiles(width, name, codes_tag)
+            nc.vector.quantize_mx(out=codes[:].bitcast(FP8X4), scales=scales[:], in_=grouped)
+            return codes, scales
+
+        def interleave(engine, grouped, raw):
+            dst = grouped.rearrange("p (c i j) -> p c j i", i=2, j=PACK)
             src = raw.rearrange("p j (c i) -> p c j i", i=2)
-            return dst, src
+            move(engine, dst, src)
 
         def multiply(bank, weights, cols, moving_words, moving_scales, start, stop):
             codes, scales = weights
@@ -92,246 +96,263 @@ def tile_moe_adp_relu2_kernel(
                 stop=stop,
             )
 
-        def bank_tag(e, t):
-            return "bank%d" % (PACK * (e % 2) + t)
-
         slot_words = {}
         slot_scales = {}
 
-        def gather(e, tag):
-            offsets = slot_tokens[:, e * C // 16 : (e + 1) * C // 16]
-            slot_words[e] = ring.tile([P, PASSES, C], U32, name=tag, align_bytes=64)
-            for s in range(PASSES):
-                nc.vector.tensor_copy(slot_words[e][:, s, :], token_words[s].bitcast(U32).indirect(offsets))
-            slot_scales[e] = ring.tile([P, C], U8, name="slot_scales%d" % e, align_bytes=64)
-            nc.vector.tensor_copy(slot_scales[e][:], token_scales[:].indirect(offsets))
+        def offsets_of(e):
+            return slot_tokens[:, e * C // 16 : (e + 1) * C // 16]
+
+        def gather_words(e, s, dst):
+            nc.vector.tensor_copy(dst, token_words[s][:].bitcast(U32).indirect(offsets_of(e)))
+            slot_words[e, s] = dst
+
+        def gather_scales(e, dst):
+            nc.vector.tensor_copy(dst, token_scales[:].indirect(offsets_of(e)))
+            slot_scales[e] = dst
+
+        def head_words(e, s):
+            tile = ring.tile([P, C], U32, name="slot_words%d_%d" % (e, s), align_bytes=64)
+            gather_words(e, s, tile[:])
+
+        def late_gathers(e):
+            base = (e - HEAD_ADAPTERS) * LATE_BYTES
+            words = late.tile([P, PASSES - 1, C], U32, name="late_words%d" % e, align_bytes=64, offset=base)
+            scales = late.tile([P, C], U8, name="late_scales%d" % e, align_bytes=64, offset=base + LATE_BYTES // 2)
+            for s in range(1, PASSES):
+                gather_words(e, s, words[:, s - 1, :])
+            gather_scales(e, scales[:])
 
         h_banks = {}
-        positive = {}
-        h_grouped = {}
         h_mx = {}
-        wb_raw = {}
-        wb_grouped = {}
-        wb_mx = {}
-        early_pairs = []
 
-        def load_wb(e):
-            wb_raw[e] = load_rows(wb[e], "wb_raw%d" % e)[:]
+        def bank_tag(e, half):
+            return "h_bank%d" % (2 * (e % 2) + half)
 
-        def round_wb(e, engine):
-            wb_grouped[e] = ring.tile([P, PACK * N], BF16, name="wb_grouped%d" % (e % 2), align_bytes=64)
-            dst, src = interleaved(wb_grouped[e], wb_raw[e])
-            round_to_bf16(engine, dst, src)
-
-        def quantize_wb(e):
-            wb_mx[e] = quantize(wb_grouped[e], N, "wb%d" % (e % 3))
-
-        def rectify(e, engines, tag):
-            positive[e] = ring.tile([P, PACK, C], F32, name=tag, align_bytes=256)
-            for t, engine in enumerate(engines):
-                if engine == "S":
-                    nc.scalar.activation(out=positive[e][:, t, :], in_=h_banks[e][t][:], func=RELU)
-                else:
-                    nc.vector.tensor_scalar_max(positive[e][:, t, :], h_banks[e][t][:], 0.0)
-
-        def square(e):
-            h_grouped[e] = ring.tile([P, PACK * C], BF16, name="h_grouped%d" % (e % 2), align_bytes=64)
-            dst, src = interleaved(h_grouped[e], positive[e][:])
-            nc.scalar.activation(out=dst, in_=src, func=SQUARE)
-
-        def quantize_h(e):
-            h_mx[e] = quantize(h_grouped[e], C, "h%d" % e)
-
-        def second_layer(e, tag):
-            h_codes, h_scales = h_mx[e]
-            y_bank = psum.tile([P, C], F32, name=tag)
-            multiply(y_bank[:], wb_mx[e], slice(0, N), h_codes[:], h_scales[:], True, True)
-            nc.scalar.copy(out=slot_results[:, e * C : (e + 1) * C], in_=y_bank[:])
-
-        def early_layer(adapters, tag, engine):
-            y_bank = psum.tile([P, len(adapters), C], F32, name=tag)
-            for a, e in enumerate(adapters):
-                h_codes, h_scales = h_mx[e]
-                multiply(y_bank[:, a, :], wb_mx["early%d" % (e // 2)], slice(a * N, (a + 1) * N), h_codes[:], h_scales[:], True, True)
-            cols = slice(adapters[0] * C, (adapters[-1] + 1) * C)
-            round_to_bf16(engine, slot_results[:, cols], y_bank[:].rearrange("p a c -> p (a c)"))
-
-        for s in range(PASSES):
-            nc.sync.dma_start(out=token_words[s], in_=x_words[s].rearrange("p t d -> p (t d)").bitcast(I32))
-            if s == 0:
-                nc.sync.dma_start(slot_tokens[:], offs)
-        for q in range(4):
-            nc.scalar.dma_start(
-                out=token_scales[32 * q : 32 * q + 4 * PASSES, :].bitcast(I32),
-                in_=x_scales[:, 4 * q : 4 * q + 4, :].bitcast(I32),
-            )
-        for e in range(FREE_GATHERS):
-            gather(e, "slot_words%d" % e)
-
-        wa_rows = wa.rearrange("e k h -> (e k) h")
-        wa_raw = []
-        raw_tags = []
-        load_count = 0
-        for chunk in range(CHUNKS - 1):
-            e, s = divmod(chunk, PASSES)
-            if chunk == len(wa_raw):
-                size = LOAD_SIZES[load_count]
-                tag = "raw%d" % (load_count % RAW_SLOTS)
-                wa_raw.extend(load_passes(wa_rows[chunk * K_PASS : (chunk + size) * K_PASS, :], tag))
-                raw_tags.extend([tag] * size)
-                load_count = load_count + 1
-            if (e, s) == (EARLY, PASSES - 1):
-                early_raw = ring.tile([P, EARLY, PACK, N], F32, name="early_raw", align_bytes=256)
-                nc.sync.dma_start(out=early_raw[:], in_=wb[0:EARLY].rearrange("e (p j) n -> p e j n", j=PACK))
-            if chunk in LATE_GATHERS:
-                grouped_tag = "slot_words%d" % LATE_GATHERS[chunk]
-            else:
-                grouped_tag = "wa_grouped%d" % (chunk % GROUP_SLOTS)
-            wa_grouped = ring.tile([P, PACK * H], BF16, name=grouped_tag, align_bytes=64)
-            if e < E - 1:
-                dst = wa_grouped[:].rearrange("p (u v m j) -> p u m j v", u=2, v=2, j=PACK)
-                src = wa_raw[chunk].rearrange("p j (m u v) -> p u m j v", u=2, v=2)
-                share = 2 * SCALAR_SHARE[chunk]
-                if share > 0:
-                    round_to_bf16("S", dst[:, :, :share], src[:, :, :share])
-                if share < P:
-                    round_to_bf16("V", dst[:, :, share:], src[:, :, share:])
-            else:
-                dst = wa_grouped[:].rearrange("p (t m r j) -> p m t j r", t=PACK, r=2, j=PACK)
-                src = wa_raw[chunk].rearrange("p j (m t r) -> p m t j r", t=PACK, r=2)
-                round_to_bf16("V", dst, src)
-            if e > 0 and s == 0:
-                behind_cast = SCALAR_SHARE[chunk] > 0
-                rectify(e - 1, "SSSS", raw_tags[chunk] if behind_cast else "early_raw")
-                square(e - 1)
-            if (e, s) == (EARLY + 1, 0):
-                early_layer([0, 1], bank_tag(e, 2), "S")
-                early_layer([2, 3], bank_tag(e, 3), "S")
-            wa_mx = quantize(wa_grouped, H, "wa%d" % (chunk % CODE_SLOTS))
-            if s == 1 and 0 < e < E - 1:
-                quantize_h(e - 1)
-            if (e, s) == (EARLY, PASSES - 1):
-                for pair, (engine, tag) in enumerate((("S", "early_grouped"), ("V", grouped_tag))):
-                    grouped = ring.tile([P, 2 * PACK * N], BF16, name=tag, align_bytes=64)
-                    round_to_bf16(
-                        engine,
-                        grouped[:].rearrange("p (e c i j) -> p e c j i", e=2, i=2, j=PACK),
-                        early_raw[:, 2 * pair : 2 * pair + 2].rearrange("p e j (c i) -> p e c j i", i=2),
-                    )
-                    early_pairs.append(grouped)
-                for pair in (1, 0):
-                    wb_mx["early%d" % pair] = quantize(early_pairs[pair], 2 * N, "early%d" % pair)
-            if chunk in LATE_GATHERS:
-                gather(LATE_GATHERS[chunk], grouped_tag)
-            if s == 0:
-                h_banks[e] = [psum.tile([P, C], F32, name=bank_tag(e, t)) for t in range(PACK)]
-            for t in range(PACK):
-                multiply(
-                    h_banks[e][t][:], wa_mx, slice(t * P, (t + 1) * P),
-                    slot_words[e][:, s, :], slot_scales[e][4 * s : P, :], s == 0, s == PASSES - 1,
-                )
-
-        e, s = E - 1, PASSES - 1
-        pair_grouped = [
-            ring.tile([P, 2 * H], BF16, name="pair_grouped%d" % pair, align_bytes=64) for pair in range(2)
-        ]
-        for half in range(2):
-            last_raw = load_rows(
-                wa[e, s * K_PASS : (s + 1) * K_PASS, half * H // 2 : (half + 1) * H // 2], "last_raw%d" % half
-            )
-            src = last_raw[:].rearrange("p j (m t r) -> p m t j r", t=PACK, r=2)
-            for pair, engine in enumerate("VS"):
-                dst = pair_grouped[pair][:].rearrange("p (t m r j) -> p m t j r", t=2, r=2, j=PACK)
-                round_to_bf16(
-                    engine, dst[:, half * P // 4 : (half + 1) * P // 4], src[:, :, 2 * pair : 2 * pair + 2]
-                )
-
-        gates = [keep.tile([P, T], F32, name="gate%d" % r) for r in range(TOP)]
-        token_slots = [keep.tile([P, T // 16], U16, name="token_slots%d" % r) for r in range(TOP)]
-        load_wb(E - 2)
-        last_wb = ring.tile([P, PACK, N], F32, name="wb_raw5", align_bytes=256)
-        rows = wb[E - 1].rearrange("(m t r) n -> r m t n", t=PACK, r=2)
-        for r in range(2):
-            nc.sync.dma_start(out=last_wb[r:P:2], in_=rows[r])
-        wb_raw[E - 1] = last_wb[:]
-        w_raw = [load_rows(w[s * K_PASS : (s + 1) * K_PASS, :], "w_raw%d" % s) for s in range(PASSES)]
-        for r, pos in enumerate((pos1, pos2, pos3)):
-            nc.sync.dma_start(token_slots[r][:], pos)
-        for r in range(TOP):
-            nc.sync.dma_start(out=gates[r][:], in_=gate[r])
-
-        s = PASSES - 1
-        for pair in range(2):
-            wa_mx = quantize(pair_grouped[pair], 2 * P, "pair%d" % pair)
-            for t in range(2):
-                multiply(
-                    h_banks[e][2 * pair + t][:], wa_mx, slice(t * P, (t + 1) * P),
-                    slot_words[e][:, s, :], slot_scales[e][4 * s : P, :], False, True,
-                )
-
-        h_codes = ring.tile([P, C], U32, name="pair_grouped0", align_bytes=64)
-        h_scales = ring.tile([P, C], U8, name="late_h_scales", align_bytes=64)
-        nc.vector.quantize_mx(out=h_codes[:].bitcast(FP8X4), scales=h_scales[:], in_=h_grouped[E - 2][:])
-        h_mx[E - 2] = (h_codes, h_scales)
-
-        def round_w(s, engine, tag):
-            grouped = ring.tile([P, PACK * N], BF16, name=tag, align_bytes=64)
-            dst, src = interleaved(grouped, w_raw[s][:])
-            round_to_bf16(engine, dst, src)
-            return grouped
-
-        def frozen_pass(s, grouped):
-            w_mx = quantize(grouped, N, "w%d" % s)
+        def first_layer(e, s, weights, t, half):
+            slots = slice(half * HALF, (half + 1) * HALF)
             multiply(
-                base_bank[:], w_mx, slice(0, N), token_words[s], token_scales[4 * s : P, :],
-                s == 0, s == PASSES - 1,
+                h_banks[e][half][:, t, :], weights, slice(t * P, (t + 1) * P),
+                slot_words[e, s][:, slots], slot_scales[e][4 * s : P, slots],
+                s == 0 and t == 0, s == PASSES - 1 and t == PACK - 1,
             )
 
-        round_wb(E - 2, "S")
-        rectify(E - 1, "SSSS", "positive0")
-        round_wb(E - 1, "V")
-        quantize_wb(E - 1)
-        halves = []
-        for half, engine in enumerate("SV"):
-            grouped = ring.tile([P, PACK * P], BF16, name="half_grouped%d" % half, align_bytes=64)
-            dst, src = interleaved(grouped, positive[E - 1][:, :, half * P : (half + 1) * P])
+        def rectify(engine, dst, bank):
+            src = bank.rearrange("p t c -> p c t")
+            dst = dst.rearrange("p (c t) -> p c t", t=PACK)
+            if engine == "S":
+                nc.scalar.activation(out=dst, in_=src, func=RELU)
+            else:
+                nc.vector.tensor_scalar_max(dst, src, 0.0)
+
+        def square(engine, dst, src):
             if engine == "S":
                 nc.scalar.activation(out=dst, in_=src, func=SQUARE)
             else:
                 nc.vector.tensor_tensor(dst, src, src, MULT)
-            halves.append(grouped)
-        quantize_wb(E - 2)
-        second_layer(E - 2, bank_tag(E - 2, 0))
-        for half in (1, 0):
-            h_codes, h_scales = quantize(halves[half], P, "half%d" % half)
-            y_bank = psum.tile([P, P], F32, name=bank_tag(E - 2, 1 + half))
+
+        def hidden(e, tag):
+            positive = ring.tile([P, PACK * C], F32, name=tag, align_bytes=256)
+            for half in range(2):
+                rectify("S", positive[:, half * PACK * HALF : (half + 1) * PACK * HALF], h_banks[e][half][:])
+            grouped = ring.tile([P, PACK * C], BF16, name="h_grouped%d" % (e % 2), align_bytes=64)
+            square("S", grouped[:], positive[:])
+            return grouped
+
+        def round_wa(engine, grouped, raw, lo, hi):
+            dst = grouped[:].rearrange("p (u v m j) -> p u m j v", u=2, v=2, j=PACK)
+            src = raw[:].rearrange("p j (m u v) -> p u m j v", u=2, v=2)
+            move(engine, dst[:, :, lo:hi], src[:, :, lo:hi])
+
+        wa_rows = wa.rearrange("e k h -> (e k) h")
+
+        def load_chunk(chunk):
+            return load_rows(wa_rows[chunk * K_PASS : (chunk + 1) * K_PASS, :], chunk)
+
+        def load_tokens(s):
+            nc.sync.dma_start(out=token_words[s][:], in_=x_words[s].rearrange("p t d -> p (t d)").bitcast(I32))
+
+        wa_raw = {}
+        load_tokens(0)
+        nc.sync.dma_start(slot_tokens[:], offs)
+        wa_raw[0] = load_chunk(0)
+        load_tokens(1)
+        wa_raw[1] = load_chunk(1)
+        for q in range(4):
+            nc.sync.dma_start(
+                out=token_scales[32 * q : 32 * q + 4 * PASSES, :].bitcast(I32),
+                in_=x_scales[:, 4 * q : 4 * q + 4, :].bitcast(I32),
+            )
+        load_tokens(2)
+        for e in range(E):
+            head_words(e, 0)
+        for s in range(1, PASSES):
+            for e in range(HEAD_ADAPTERS):
+                head_words(e, s)
+        for e in range(HEAD_ADAPTERS):
+            tile = ring.tile([P, C], U8, name="slot_scales%d" % e, align_bytes=64)
+            gather_scales(e, tile[:])
+
+        h_grouped = {}
+        waiting = {}
+        for chunk in range(CHUNKS - 1):
+            e, s = divmod(chunk, PASSES)
+            if chunk not in wa_raw:
+                wa_raw[chunk] = load_chunk(chunk)
+            holds_gathers = s == PASSES - 1 and 1 <= e <= E - HEAD_ADAPTERS
+            if holds_gathers:
+                grouped = late.tile(
+                    [P, PACK * H], BF16, name="late_grouped%d" % e, align_bytes=64, offset=(e - 1) * LATE_BYTES
+                )
+            else:
+                grouped = ring.tile([P, PACK * H], BF16, name="wa_grouped%d" % (chunk % GROUP_SLOTS), align_bytes=64)
+            share = SCALAR_SHARE[chunk]
+            if share > 0:
+                round_wa("S", grouped, wa_raw[chunk], 0, share)
+            if share < P:
+                round_wa("V", grouped, wa_raw[chunk], share, P)
+            if chunk in RELU_BEHIND:
+                h_grouped[e - 1] = hidden(e - 1, "raw%d" % (chunk % RAW_SLOTS))
+            if s == PASSES - 1 and e > 0:
+                h_mx[e - 1] = quantize(h_grouped[e - 1][:], C, "h%d" % (e - 1))
+            if s == 0:
+                h_banks[e] = [psum.tile([P, PACK, HALF], F32, name=bank_tag(e, half)) for half in range(2)]
+            waiting[s] = grouped
+            if s == 0 and 1 < e < E - 1:
+                continue
+            for k in sorted(waiting):
+                name = "wa%d" % ((chunk - s + k) % CODE_SLOTS)
+                if k < s:
+                    codes = ring.tile([P, H], U32, name="raw%d" % (chunk % RAW_SLOTS), align_bytes=256)
+                    scales = ring.tile([P, H], U8, name=name + "_scales", align_bytes=64)
+                    nc.vector.quantize_mx(out=codes[:].bitcast(FP8X4), scales=scales[:], in_=waiting[k][:])
+                    wa_mx = (codes, scales)
+                else:
+                    wa_mx = quantize(waiting[k][:], H, name)
+                    if holds_gathers:
+                        late_gathers(e + HEAD_ADAPTERS - 1)
+                for half in range(2):
+                    for t in range(PACK):
+                        first_layer(e, k, wa_mx, t, half)
+            waiting.clear()
+            if (e, s) == (E - 2, PASSES - 1):
+                early_raw = ring.tile([P, EARLY, PACK, N], F32, name="early_raw", align_bytes=256)
+                nc.sync.dma_start(out=early_raw[:], in_=wb[0:EARLY].rearrange("e (p j) n -> p e j n", j=PACK))
+                for r, pos in enumerate((pos1, pos2, pos3)):
+                    nc.sync.dma_start(token_slots[r][:], pos)
+                early_mx = {}
+                early_grouped = {}
+                for pair, engine in enumerate("SV"):
+                    early_grouped[pair] = ring.tile([P, 2 * PACK * N], BF16, name="early_grouped%d" % pair, align_bytes=64)
+                    move(
+                        engine,
+                        early_grouped[pair][:].rearrange("p (e c i j) -> p e c j i", e=2, i=2, j=PACK),
+                        early_raw[:, 2 * pair : 2 * pair + 2].rearrange("p e j (c i) -> p e c j i", i=2),
+                    )
+                h_grouped[e] = hidden(e, "early_raw")
+                for pair, engine in ((1, "S"), (0, "S")):
+                    early_mx[pair] = quantize(early_grouped[pair][:], 2 * N, "early%d" % pair)
+                    y_bank = psum.tile([P, 2, C], F32, name="y_bank%d" % pair)
+                    for a in range(2):
+                        h_codes, h_scales = h_mx[2 * pair + a]
+                        multiply(y_bank[:, a, :], early_mx[pair], slice(a * N, (a + 1) * N), h_codes[:], h_scales[:], True, True)
+                    move(
+                        engine, slot_results[:, 2 * pair * C : (2 * pair + 2) * C], y_bank[:].rearrange("p a c -> p (a c)")
+                    )
+            if (e, s) == (E - 1, 0):
+                h_mx[e - 1] = quantize(h_grouped[e - 1][:], C, "h%d" % (e - 1), "wa_grouped%d" % (chunk % GROUP_SLOTS))
+
+        e, s = E - 1, PASSES - 1
+        last_raw = load_chunk(CHUNKS - 1)
+        slot = CHUNKS + 1
+        wb_raw = {a: load_rows(wb[a], slot + E - 1 - a) for a in (E - 1, E - 2)}
+        w_raw = [load_rows(w[k * K_PASS : (k + 1) * K_PASS, :], slot + 2 + k) for k in range(PASSES)]
+        gates = {}
+        for r in (2, 0, 1):
+            gates[r] = raw_tile([P, T], slot + 5 + r)
+            nc.sync.dma_start(out=gates[r][:], in_=gate[r])
+
+        grouped = ring.tile([P, PACK * H], BF16, name="wa_grouped%d" % ((CHUNKS - 1) % GROUP_SLOTS), align_bytes=64)
+        dst = grouped[:].rearrange("p (u v m j) -> p u m j v", u=2, v=2, j=PACK)
+        src = last_raw[:].rearrange("p j (m u v) -> p u m j v", u=2, v=2)
+        move("V", dst[:, 0], src[:, 0])
+        move("S", dst[:, 1, :SPLIT_17B], src[:, 1, :SPLIT_17B])
+        move("V", dst[:, 1, SPLIT_17B:], src[:, 1, SPLIT_17B:])
+        wa_mx = mx_tiles(H, "wa%d" % ((CHUNKS - 1) % CODE_SLOTS))
+        for t in range(PACK):
+            cols = slice(t * P, (t + 1) * P)
+            nc.vector.quantize_mx(
+                out=wa_mx[0][:, cols].bitcast(FP8X4), scales=wa_mx[1][:, cols], in_=grouped[:, t * K_PASS : (t + 1) * K_PASS]
+            )
+        for t, half in ((0, 0), (0, 1), (1, 0), (1, 1), (2, 0), (3, 0), (2, 1), (3, 1)):
+            first_layer(e, s, wa_mx, t, half)
+
+        wb_grouped = {}
+        wb_mx = {}
+        for a, engine in ((E - 1, "S"), (E - 2, "V")):
+            wb_grouped[a] = ring.tile([P, PACK * N], BF16, name="wb_grouped%d" % a, align_bytes=64)
+            interleave(engine, wb_grouped[a][:], wb_raw[a][:])
+        for a in (E - 1, E - 2):
+            wb_mx[a] = quantize(wb_grouped[a][:], N, "wb%d" % a)
+
+        positive = []
+        halves = []
+        for half, engine in enumerate("SV"):
+            positive.append(ring.tile([P, PACK * HALF], F32, name="last_positive%d" % half, align_bytes=64))
+            halves.append(ring.tile([P, PACK * HALF], BF16, name="last_grouped%d" % half, align_bytes=64))
+            for part in range(2):
+                cols = slice(part * 2 * HALF, (part + 1) * 2 * HALF)
+                rectify(engine, positive[half][:, cols], h_banks[e][half][:, :, part * HALF // 2 : (part + 1) * HALF // 2])
+            for part in range(2):
+                cols = slice(part * 2 * HALF, (part + 1) * 2 * HALF)
+                square(engine, halves[half][:, cols], positive[half][:, cols])
+
+        y_bank = psum.tile([P, C], F32, name="y_bank0")
+        h_codes, h_scales = h_mx[E - 2]
+        multiply(y_bank[:], wb_mx[E - 2], slice(0, N), h_codes[:], h_scales[:], True, True)
+        move("S", slot_results[:, (E - 2) * C : (E - 1) * C], y_bank[:])
+
+        for half in range(2):
+            h_codes, h_scales = quantize(halves[half][:], HALF, "half%d" % half)
+            y_bank = psum.tile([P, HALF], F32, name=bank_tag(E - 2, half))
             multiply(y_bank[:], wb_mx[E - 1], slice(0, N), h_codes[:], h_scales[:], True, True)
-            first_slot = (E - 1) * C + half * P
-            nc.scalar.copy(out=slot_results[:, first_slot : first_slot + P], in_=y_bank[:])
+            first_slot = (E - 1) * C + half * HALF
+            move("S", slot_results[:, first_slot : first_slot + HALF], y_bank[:])
 
-        base_bank = psum.tile([P, T], F32, name=bank_tag(E - 2, 3))
-        w_tags = ["last_term%d" % r for r in range(TOP)]
-        for s in range(PASSES):
-            frozen_pass(s, round_w(s, "VVS"[s], "w_grouped%d" % s))
+        base_bank = psum.tile([P, T], F32, name="base_bank")
+        for k, (engine, tag) in enumerate((("S", "last_positive0"), ("V", "last_positive1"), ("V", "last_grouped1"))):
+            w_grouped = ring.tile([P, PACK * N], BF16, name=tag, align_bytes=64)
+            interleave(engine, w_grouped[:], w_raw[k][:])
+            w_mx = quantize(w_grouped[:], N, "w%d" % k)
+            multiply(
+                base_bank[:], w_mx, slice(0, N), token_words[k][:], token_scales[4 * k : P, :], k == 0, k == PASSES - 1
+            )
 
-        def weighted(r, start, stop, tag):
-            term = ring.tile([P, stop - start], F32, name=tag, align_bytes=64)
-            offsets = token_slots[r][:, start // 16 : stop // 16]
-            nc.vector.tensor_tensor(term[:], slot_results[:].indirect(offsets), gates[r][:, start:stop], MULT)
-            return term
+        groups = ((0, FIRST_TOKENS), (FIRST_TOKENS, T))
 
-        def add(a, b, name):
-            total = ring.tile(list(a.shape), F32, name=name, align_bytes=64)
-            nc.vector.tensor_tensor(total[:], a, b, ADD)
-            return total
+        def term_tile(g, name):
+            return ring.tile([P, groups[g][1] - groups[g][0]], F32, name="%s%d" % (name, g), align_bytes=64)
 
-        first_terms = [weighted(r, 0, FIRST_TOKENS, "wa_grouped%d" % r) for r in range(TOP)]
-        first_sum = add(first_terms[0][:], first_terms[1][:], "slot_words0")
-        first_base = add(first_terms[2][:], base_bank[:, 0:FIRST_TOKENS], "slot_words1")
-        last_terms = [weighted(r, FIRST_TOKENS, T, w_tags[r]) for r in range(TOP)]
-        first_sum = add(first_sum[:], first_base[:], "slot_words2")
-        nc.sync.dma_start(out=out[:, 0:FIRST_TOKENS], in_=first_sum[:])
-        last_pair = add(last_terms[0][:], last_terms[1][:], "last_pair")
-        last_base = add(last_terms[2][:], base_bank[:, FIRST_TOKENS:T], "last_base")
-        last_sum = add(last_pair[:], last_base[:], "last_total")
-        nc.sync.dma_start(out=out[:, FIRST_TOKENS:T], in_=last_sum[:])
+        def window(r, g):
+            return slot_results[:].indirect(token_slots[r][:, groups[g][0] // 16 : groups[g][1] // 16])
+
+        def combine(g, name, a, b, op):
+            total = term_tile(g, name)
+            nc.vector.tensor_tensor(total[:], a, b, op)
+            return total[:]
+
+        picked = {}
+        for g in range(2):
+            for r in range(2):
+                picked[r, g] = term_tile(g, "picked%d_" % r)
+                nc.scalar.activation(picked[r, g][:], window(r, g), COPY)
+        third = [combine(g, "third", window(2, g), gates[2][:, slice(*groups[g])], MULT) for g in range(2)]
+        first = [None, None]
+        first[0] = combine(0, "first", picked[0, 0][:], gates[0][:, slice(*groups[0])], MULT)
+        for g in range(2):
+            with_base = combine(g, "with_base", third[g], base_bank[:, slice(*groups[g])], ADD)
+            second = combine(g, "second", picked[1, g][:], gates[1][:, slice(*groups[g])], MULT)
+            partial = combine(g, "partial", first[g], with_base, ADD)
+            if g == 0:
+                first[1] = combine(1, "first", picked[0, 1][:], gates[0][:, slice(*groups[1])], MULT)
+            total = combine(g, "total", partial, second, ADD)
+            nc.sync.dma_start(out=out[:, slice(*groups[g])], in_=total)

@@ -171,17 +171,21 @@ def tile_moe_adp_relu2_kernel(
         def load_tokens(s):
             nc.sync.dma_start(out=token_words[s][:], in_=x_words[s].rearrange("p t d -> p (t d)").bitcast(I32))
 
+        def load_scales(first, last):
+            for q in range(4):
+                nc.sync.dma_start(
+                    out=token_scales[32 * q + 4 * first : 32 * q + 4 * last, :].bitcast(I32),
+                    in_=x_scales[first:last, 4 * q : 4 * q + 4, :].bitcast(I32),
+                )
+
         wa_raw = {}
         load_tokens(0)
         nc.sync.dma_start(slot_tokens[:], offs)
         wa_raw[0] = load_chunk(0)
+        load_scales(0, 2)
         load_tokens(1)
         wa_raw[1] = load_chunk(1)
-        for q in range(4):
-            nc.sync.dma_start(
-                out=token_scales[32 * q : 32 * q + 4 * PASSES, :].bitcast(I32),
-                in_=x_scales[:, 4 * q : 4 * q + 4, :].bitcast(I32),
-            )
+        load_scales(2, 3)
         load_tokens(2)
         for e in range(E):
             head_words(e, 0)

@@ -1,6 +1,7 @@
 from contextlib import ExitStack
 
 import concourse.mybir as mybir
+from concourse.masks import make_identity
 
 K, T, E, C, H, N, TOP = 1536, 512, 6, 256, 512, 128, 3
 P = 128
@@ -54,6 +55,8 @@ def tile_moe_adp_relu2_kernel(
         token_words = [keep.tile([P, T], I32, name="token_words%d" % s, align_bytes=256) for s in range(PASSES)]
         slot_results = keep.tile([P, SLOTS], F32, name="slot_results", align_bytes=64)
         nc.gpsimd.memset(token_scales[:].bitcast(I32), 0)
+        identity = keep.tile([P, P], F32, name="identity")
+        make_identity(nc, identity[:])
 
         def move(engine, dst, src):
             if engine == "S":
@@ -270,10 +273,13 @@ def tile_moe_adp_relu2_kernel(
         slot = CHUNKS + 1
         wb_raw = {a: load_rows(wb[a], slot + E - 1 - a) for a in (E - 1, E - 2)}
         w_raw = [load_rows(w[k * K_PASS : (k + 1) * K_PASS, :], slot + 2 + k) for k in range(PASSES)]
-        gates = {}
-        for r in (2, 0, 1):
-            gates[r] = raw_tile([P, T], slot + 5 + r)
-            nc.sync.dma_start(out=gates[r][:], in_=gate[r])
+        groups = ((0, FIRST_TOKENS), (FIRST_TOKENS, T))
+        last_gate = raw_tile([P, T], slot + 5)
+        nc.sync.dma_start(out=last_gate[:], in_=gate[TOP - 1])
+        gates = []
+        for g, (first, end) in enumerate(groups):
+            gates.append(raw_tile([P, TOP - 1, end - first], slot + 6 + g))
+            nc.sync.dma_start(out=gates[g][:], in_=gate[: TOP - 1, :, first:end].rearrange("r p t -> p r t"))
 
         grouped = ring.tile([P, PACK * H], BF16, name="wa_grouped%d" % ((CHUNKS - 1) % GROUP_SLOTS), align_bytes=64)
         dst = grouped[:].rearrange("p (u v m j) -> p u m j v", u=2, v=2, j=PACK)
@@ -322,16 +328,18 @@ def tile_moe_adp_relu2_kernel(
             first_slot = (E - 1) * C + half * HALF
             move("S", slot_results[:, first_slot : first_slot + HALF], y_bank[:])
 
-        base_bank = psum.tile([P, T], F32, name="base_bank")
+        base_banks = [psum.tile([P, end - first], F32, name="base_bank%d" % g) for g, (first, end) in enumerate(groups)]
+        w_mx = []
         for k, (engine, tag) in enumerate((("S", "last_positive0"), ("V", "last_positive1"), ("V", "last_grouped1"))):
             w_grouped = ring.tile([P, PACK * N], BF16, name=tag, align_bytes=64)
             interleave(engine, w_grouped[:], w_raw[k][:])
-            w_mx = quantize(w_grouped[:], N, "w%d" % k)
-            multiply(
-                base_bank[:], w_mx, slice(0, N), token_words[k][:], token_scales[4 * k : P, :], k == 0, k == PASSES - 1
-            )
-
-        groups = ((0, FIRST_TOKENS), (FIRST_TOKENS, T))
+            w_mx.append(quantize(w_grouped[:], N, "w%d" % k))
+        for g, (first, end) in enumerate(groups):
+            for k in range(PASSES):
+                multiply(
+                    base_banks[g][:], w_mx[k], slice(0, N), token_words[k][:, first:end],
+                    token_scales[4 * k : P, first:end], k == 0, k == PASSES - 1,
+                )
 
         def term_tile(g, name):
             return ring.tile([P, groups[g][1] - groups[g][0]], F32, name="%s%d" % (name, g), align_bytes=64)
@@ -349,14 +357,39 @@ def tile_moe_adp_relu2_kernel(
             for r in range(2):
                 picked[r, g] = term_tile(g, "picked%d_" % r)
                 nc.scalar.activation(picked[r, g][:], window(r, g), COPY)
-        third = [combine(g, "third", window(2, g), gates[2][:, slice(*groups[g])], MULT) for g in range(2)]
-        first = [None, None]
-        first[0] = combine(0, "first", picked[0, 0][:], gates[0][:, slice(*groups[0])], MULT)
-        for g in range(2):
-            with_base = combine(g, "with_base", third[g], base_bank[:, slice(*groups[g])], ADD)
-            second = combine(g, "second", picked[1, g][:], gates[1][:, slice(*groups[g])], MULT)
-            partial = combine(g, "partial", first[g], with_base, ADD)
-            if g == 0:
-                first[1] = combine(1, "first", picked[0, 1][:], gates[0][:, slice(*groups[1])], MULT)
-            total = combine(g, "total", partial, second, ADD)
-            nc.sync.dma_start(out=out[:, slice(*groups[g])], in_=total)
+        def weighted(r, g):
+            return combine(g, "weighted%d_" % r, picked[r, g][:], gates[g][:, r, :], MULT)
+
+        def fused(g):
+            third = combine(g, "third", window(2, g), last_gate[:, slice(*groups[g])], MULT)
+            return third
+
+        def with_base(g, third):
+            return combine(g, "with_base", third, base_banks[g][:], ADD)
+
+        thirds = [fused(0), fused(1)]
+        terms = [weighted(0, 0), weighted(1, 0)]
+        terms.append(with_base(0, thirds[0]))
+        blocks = FIRST_TOKENS // P
+        turned_bank = psum.tile([P, blocks, P], F32, name=bank_tag(E - 1, 0))
+        for i, term in enumerate(terms):
+            for c in range(blocks):
+                nc.tensor.matmul(
+                    turned_bank[:, c, :], term[:, c * P : (c + 1) * P], identity[:], is_transpose=True,
+                    start=i == 0 and c == 0, stop=i == len(terms) - 1 and c == blocks - 1,
+                )
+        turned = term_tile(0, "turned")
+        move("S", turned[:], turned_bank[:].rearrange("p c n -> p (c n)"))
+        back_bank = psum.tile([P, blocks, P], F32, name=bank_tag(E - 1, 1))
+        for c in range(blocks):
+            nc.tensor.transpose(back_bank[:, c, :], turned[:, c * P : (c + 1) * P], identity[:])
+        total = term_tile(0, "total")
+        move("S", total[:], back_bank[:].rearrange("p c n -> p (c n)"))
+        nc.sync.dma_start(out=out[:, slice(*groups[0])], in_=total[:])
+
+        first = weighted(0, 1)
+        based = with_base(1, thirds[1])
+        second = weighted(1, 1)
+        partial = combine(1, "partial", first, based, ADD)
+        total = combine(1, "total", partial, second, ADD)
+        nc.sync.dma_start(out=out[:, slice(*groups[1])], in_=total)

from contextlib import ExitStack

import concourse.mybir as mybir
from concourse.masks import make_identity

K, T, E, C, H, N, TOP = 1536, 512, 6, 256, 512, 128, 3
P = 128
PACK = 4
K_PASS = P * PACK
PASSES = K // K_PASS
SLOTS = E * C
CHUNKS = E * PASSES

FLOPS = 2 * K * N * T + 2 * SLOTS * K * H + 2 * SLOTS * H * N

F32 = mybir.dt.float32
BF16 = mybir.dt.bfloat16
I32 = mybir.dt.int32
U32 = mybir.dt.uint32
U16 = mybir.dt.uint16
U8 = mybir.dt.uint8
FP8X4 = mybir.dt.float8_e4m3fn_x4
MULT = mybir.AluOpType.mult
ADD = mybir.AluOpType.add
RELU = mybir.ActivationFunctionType.Relu
SQUARE = mybir.ActivationFunctionType.Square
COPY = mybir.ActivationFunctionType.Copy

RAW_SLOTS = 12
GROUP_SLOTS = 4
CODE_SLOTS = 6
HEAD_ADAPTERS = 3
EARLY = 4
HALF = C // 2
SCALAR_SHARE = [128] * 4 + [88, 0] + [128, 0, 68] * 2 + [128, 0, 30] + [0, 44]
RELU_BEHIND = (4, 6, 9, 12)
SPLIT_17B = 88
FIRST_TOKENS = 256
LATE_BYTES = PACK * H * 2


def tile_moe_adp_relu2_kernel(
    tc, x_words, x_scales, w, wa, wb, gate, offs, pos1, pos2, pos3, out
):
    nc = tc.nc
    with ExitStack() as ctx:
        keep = ctx.enter_context(tc.tile_pool(name="keep", bufs=1))
        ring = ctx.enter_context(tc.tile_pool(name="ring", bufs=1))
        late = ctx.enter_context(tc.tile_pool(name="late", bufs=1))
        psum = ctx.enter_context(tc.psum_pool(name="psum", bufs=1))

        slot_tokens = keep.tile([P, SLOTS // 16], U16, name="slot_tokens")
        token_slots = [keep.tile([P, T // 16], U16, name="token_slots%d" % r) for r in range(TOP)]
        token_scales = keep.tile([P, T], U8, name="token_scales", align_bytes=64)
        token_words = [keep.tile([P, T], I32, name="token_words%d" % s, align_bytes=256) for s in range(PASSES)]
        slot_results = keep.tile([P, SLOTS], F32, name="slot_results", align_bytes=64)
        nc.gpsimd.memset(token_scales[:].bitcast(I32), 0)
        identity = keep.tile([P, P], F32, name="identity")
        make_identity(nc, identity[:])

        def move(engine, dst, src):
            if engine == "S":
                nc.scalar.copy(out=dst, in_=src)
            else:
                nc.vector.tensor_copy(out=dst, in_=src)

        def raw_tile(shape, slot):
            return ring.tile(shape, F32, name="raw%d" % (slot % RAW_SLOTS), align_bytes=256)

        def load_rows(rows, slot):
            raw = raw_tile([P, PACK, rows.shape[1]], slot)
            nc.sync.dma_start(out=raw[:], in_=rows.rearrange("(p j) c -> p j c", j=PACK))
            return raw

        def mx_tiles(width, name, codes_tag=None):
            codes = ring.tile([P, width], U32, name=codes_tag or name + "_codes", align_bytes=64)
            scales = ring.tile([P, width], U8, name=name + "_scales", align_bytes=64)
            return codes, scales

        def quantize(grouped, width, name, codes_tag=None):
            codes, scales = mx_tiles(width, name, codes_tag)
            nc.vector.quantize_mx(out=codes[:].bitcast(FP8X4), scales=scales[:], in_=grouped)
            return codes, scales

        def interleave(engine, grouped, raw):
            dst = grouped.rearrange("p (c i j) -> p c j i", i=2, j=PACK)
            src = raw.rearrange("p j (c i) -> p c j i", i=2)
            move(engine, dst, src)

        def multiply(bank, weights, cols, moving_words, moving_scales, start, stop):
            codes, scales = weights
            nc.tensor.matmul_mx(
                out=bank,
                lhsT=codes[:, cols].bitcast(FP8X4),
                lhsT_scale=scales[:, cols],
                rhs=moving_words.bitcast(FP8X4),
                rhs_scale=moving_scales,
                start=start,
                stop=stop,
            )

        slot_words = {}
        slot_scales = {}

        def offsets_of(e):
            return slot_tokens[:, e * C // 16 : (e + 1) * C // 16]

        def gather_words(e, s, dst):
            nc.vector.tensor_copy(dst, token_words[s][:].bitcast(U32).indirect(offsets_of(e)))
            slot_words[e, s] = dst

        def gather_scales(e, dst):
            nc.vector.tensor_copy(dst, token_scales[:].indirect(offsets_of(e)))
            slot_scales[e] = dst

        def head_words(e, s):
            tile = ring.tile([P, C], U32, name="slot_words%d_%d" % (e, s), align_bytes=64)
            gather_words(e, s, tile[:])

        def late_gathers(e):
            base = (e - HEAD_ADAPTERS) * LATE_BYTES
            words = late.tile([P, PASSES - 1, C], U32, name="late_words%d" % e, align_bytes=64, offset=base)
            scales = late.tile([P, C], U8, name="late_scales%d" % e, align_bytes=64, offset=base + LATE_BYTES // 2)
            for s in range(1, PASSES):
                gather_words(e, s, words[:, s - 1, :])
            gather_scales(e, scales[:])

        h_banks = {}
        h_mx = {}

        def bank_tag(e, half):
            return "h_bank%d" % (2 * (e % 2) + half)

        def first_layer(e, s, weights, t, half):
            slots = slice(half * HALF, (half + 1) * HALF)
            multiply(
                h_banks[e][half][:, t, :], weights, slice(t * P, (t + 1) * P),
                slot_words[e, s][:, slots], slot_scales[e][4 * s : P, slots],
                s == 0 and t == 0, s == PASSES - 1 and t == PACK - 1,
            )

        def rectify(engine, dst, bank):
            src = bank.rearrange("p t c -> p c t")
            dst = dst.rearrange("p (c t) -> p c t", t=PACK)
            if engine == "S":
                nc.scalar.activation(out=dst, in_=src, func=RELU)
            else:
                nc.vector.tensor_scalar_max(dst, src, 0.0)

        def square(engine, dst, src):
            if engine == "S":
                nc.scalar.activation(out=dst, in_=src, func=SQUARE)
            else:
                nc.vector.tensor_tensor(dst, src, src, MULT)

        def hidden(e, tag):
            positive = ring.tile([P, PACK * C], F32, name=tag, align_bytes=256)
            for half in range(2):
                rectify("S", positive[:, half * PACK * HALF : (half + 1) * PACK * HALF], h_banks[e][half][:])
            grouped = ring.tile([P, PACK * C], BF16, name="h_grouped%d" % (e % 2), align_bytes=64)
            square("S", grouped[:], positive[:])
            return grouped

        def round_wa(engine, grouped, raw, lo, hi):
            dst = grouped[:].rearrange("p (u v m j) -> p u m j v", u=2, v=2, j=PACK)
            src = raw[:].rearrange("p j (m u v) -> p u m j v", u=2, v=2)
            move(engine, dst[:, :, lo:hi], src[:, :, lo:hi])

        wa_rows = wa.rearrange("e k h -> (e k) h")

        def load_chunk(chunk):
            return load_rows(wa_rows[chunk * K_PASS : (chunk + 1) * K_PASS, :], chunk)

        def load_tokens(s):
            nc.sync.dma_start(out=token_words[s][:], in_=x_words[s].rearrange("p t d -> p (t d)").bitcast(I32))

        def load_scales(first, last):
            for q in range(4):
                nc.sync.dma_start(
                    out=token_scales[32 * q + 4 * first : 32 * q + 4 * last, :].bitcast(I32),
                    in_=x_scales[first:last, 4 * q : 4 * q + 4, :].bitcast(I32),
                )

        wa_raw = {}
        load_tokens(0)
        nc.sync.dma_start(slot_tokens[:], offs)
        wa_raw[0] = load_chunk(0)
        load_scales(0, 2)
        load_tokens(1)
        wa_raw[1] = load_chunk(1)
        load_scales(2, 3)
        load_tokens(2)
        for e in range(E):
            head_words(e, 0)
        for s in range(1, PASSES):
            for e in range(HEAD_ADAPTERS):
                head_words(e, s)
        for e in range(HEAD_ADAPTERS):
            tile = ring.tile([P, C], U8, name="slot_scales%d" % e, align_bytes=64)
            gather_scales(e, tile[:])

        h_grouped = {}
        waiting = {}
        for chunk in range(CHUNKS - 1):
            e, s = divmod(chunk, PASSES)
            if chunk not in wa_raw:
                wa_raw[chunk] = load_chunk(chunk)
            holds_gathers = s == PASSES - 1 and 1 <= e <= E - HEAD_ADAPTERS
            if holds_gathers:
                grouped = late.tile(
                    [P, PACK * H], BF16, name="late_grouped%d" % e, align_bytes=64, offset=(e - 1) * LATE_BYTES
                )
            else:
                grouped = ring.tile([P, PACK * H], BF16, name="wa_grouped%d" % (chunk % GROUP_SLOTS), align_bytes=64)
            share = SCALAR_SHARE[chunk]
            if share > 0:
                round_wa("S", grouped, wa_raw[chunk], 0, share)
            if share < P:
                round_wa("V", grouped, wa_raw[chunk], share, P)
            if chunk in RELU_BEHIND:
                h_grouped[e - 1] = hidden(e - 1, "raw%d" % (chunk % RAW_SLOTS))
            if s == PASSES - 1 and e > 0:
                h_mx[e - 1] = quantize(h_grouped[e - 1][:], C, "h%d" % (e - 1))
            if s == 0:
                h_banks[e] = [psum.tile([P, PACK, HALF], F32, name=bank_tag(e, half)) for half in range(2)]
            waiting[s] = grouped
            if s == 0 and 1 < e < E - 1:
                continue
            for k in sorted(waiting):
                name = "wa%d" % ((chunk - s + k) % CODE_SLOTS)
                if k < s:
                    codes = ring.tile([P, H], U32, name="raw%d" % (chunk % RAW_SLOTS), align_bytes=256)
                    scales = ring.tile([P, H], U8, name=name + "_scales", align_bytes=64)
                    nc.vector.quantize_mx(out=codes[:].bitcast(FP8X4), scales=scales[:], in_=waiting[k][:])
                    wa_mx = (codes, scales)
                else:
                    wa_mx = quantize(waiting[k][:], H, name)
                    if holds_gathers:
                        late_gathers(e + HEAD_ADAPTERS - 1)
                for half in range(2):
                    for t in range(PACK):
                        first_layer(e, k, wa_mx, t, half)
            waiting.clear()
            if (e, s) == (E - 2, PASSES - 1):
                early_raw = ring.tile([P, EARLY, PACK, N], F32, name="early_raw", align_bytes=256)
                nc.sync.dma_start(out=early_raw[:], in_=wb[0:EARLY].rearrange("e (p j) n -> p e j n", j=PACK))
                for r, pos in enumerate((pos1, pos2, pos3)):
                    nc.sync.dma_start(token_slots[r][:], pos)
                early_mx = {}
                early_grouped = {}
                for pair, engine in enumerate("SV"):
                    early_grouped[pair] = ring.tile([P, 2 * PACK * N], BF16, name="early_grouped%d" % pair, align_bytes=64)
                    move(
                        engine,
                        early_grouped[pair][:].rearrange("p (e c i j) -> p e c j i", e=2, i=2, j=PACK),
                        early_raw[:, 2 * pair : 2 * pair + 2].rearrange("p e j (c i) -> p e c j i", i=2),
                    )
                h_grouped[e] = hidden(e, "early_raw")
                for pair, engine in ((1, "S"), (0, "S")):
                    early_mx[pair] = quantize(early_grouped[pair][:], 2 * N, "early%d" % pair)
                    y_bank = psum.tile([P, 2, C], F32, name="y_bank%d" % pair)
                    for a in range(2):
                        h_codes, h_scales = h_mx[2 * pair + a]
                        multiply(y_bank[:, a, :], early_mx[pair], slice(a * N, (a + 1) * N), h_codes[:], h_scales[:], True, True)
                    move(
                        engine, slot_results[:, 2 * pair * C : (2 * pair + 2) * C], y_bank[:].rearrange("p a c -> p (a c)")
                    )
            if (e, s) == (E - 1, 0):
                h_mx[e - 1] = quantize(h_grouped[e - 1][:], C, "h%d" % (e - 1), "wa_grouped%d" % (chunk % GROUP_SLOTS))

        e, s = E - 1, PASSES - 1
        last_raw = load_chunk(CHUNKS - 1)
        slot = CHUNKS + 1
        wb_raw = {a: load_rows(wb[a], slot + E - 1 - a) for a in (E - 1, E - 2)}
        w_raw = [load_rows(w[k * K_PASS : (k + 1) * K_PASS, :], slot + 2 + k) for k in range(PASSES)]
        groups = ((0, FIRST_TOKENS), (FIRST_TOKENS, T))
        last_gate = raw_tile([P, T], slot + 5)
        nc.sync.dma_start(out=last_gate[:], in_=gate[TOP - 1])
        gates = []
        for g, (first, end) in enumerate(groups):
            gates.append(raw_tile([P, TOP - 1, end - first], slot + 6 + g))
            nc.sync.dma_start(out=gates[g][:], in_=gate[: TOP - 1, :, first:end].rearrange("r p t -> p r t"))

        grouped = ring.tile([P, PACK * H], BF16, name="wa_grouped%d" % ((CHUNKS - 1) % GROUP_SLOTS), align_bytes=64)
        dst = grouped[:].rearrange("p (u v m j) -> p u m j v", u=2, v=2, j=PACK)
        src = last_raw[:].rearrange("p j (m u v) -> p u m j v", u=2, v=2)
        move("V", dst[:, 0], src[:, 0])
        move("S", dst[:, 1, :SPLIT_17B], src[:, 1, :SPLIT_17B])
        move("V", dst[:, 1, SPLIT_17B:], src[:, 1, SPLIT_17B:])
        wa_mx = mx_tiles(H, "wa%d" % ((CHUNKS - 1) % CODE_SLOTS))
        for t in range(PACK):
            cols = slice(t * P, (t + 1) * P)
            nc.vector.quantize_mx(
                out=wa_mx[0][:, cols].bitcast(FP8X4), scales=wa_mx[1][:, cols], in_=grouped[:, t * K_PASS : (t + 1) * K_PASS]
            )
        for t, half in ((0, 0), (0, 1), (1, 0), (1, 1), (2, 0), (3, 0), (2, 1), (3, 1)):
            first_layer(e, s, wa_mx, t, half)

        wb_grouped = {}
        wb_mx = {}
        for a, engine in ((E - 1, "S"), (E - 2, "V")):
            wb_grouped[a] = ring.tile([P, PACK * N], BF16, name="wb_grouped%d" % a, align_bytes=64)
            interleave(engine, wb_grouped[a][:], wb_raw[a][:])
        for a in (E - 1, E - 2):
            wb_mx[a] = quantize(wb_grouped[a][:], N, "wb%d" % a)

        positive = []
        halves = []
        for half, engine in enumerate("SV"):
            positive.append(ring.tile([P, PACK * HALF], F32, name="last_positive%d" % half, align_bytes=64))
            halves.append(ring.tile([P, PACK * HALF], BF16, name="last_grouped%d" % half, align_bytes=64))
            for part in range(2):
                cols = slice(part * 2 * HALF, (part + 1) * 2 * HALF)
                rectify(engine, positive[half][:, cols], h_banks[e][half][:, :, part * HALF // 2 : (part + 1) * HALF // 2])
            for part in range(2):
                cols = slice(part * 2 * HALF, (part + 1) * 2 * HALF)
                square(engine, halves[half][:, cols], positive[half][:, cols])

        y_bank = psum.tile([P, C], F32, name="y_bank0")
        h_codes, h_scales = h_mx[E - 2]
        multiply(y_bank[:], wb_mx[E - 2], slice(0, N), h_codes[:], h_scales[:], True, True)
        move("S", slot_results[:, (E - 2) * C : (E - 1) * C], y_bank[:])

        for half in range(2):
            h_codes, h_scales = quantize(halves[half][:], HALF, "half%d" % half)
            y_bank = psum.tile([P, HALF], F32, name=bank_tag(E - 2, half))
            multiply(y_bank[:], wb_mx[E - 1], slice(0, N), h_codes[:], h_scales[:], True, True)
            first_slot = (E - 1) * C + half * HALF
            move("S", slot_results[:, first_slot : first_slot + HALF], y_bank[:])

        base_banks = [psum.tile([P, end - first], F32, name="base_bank%d" % g) for g, (first, end) in enumerate(groups)]
        w_mx = []
        for k, (engine, tag) in enumerate((("S", "last_positive0"), ("V", "last_positive1"), ("V", "last_grouped1"))):
            w_grouped = ring.tile([P, PACK * N], BF16, name=tag, align_bytes=64)
            interleave(engine, w_grouped[:], w_raw[k][:])
            w_mx.append(quantize(w_grouped[:], N, "w%d" % k))
        for g, (first, end) in enumerate(groups):
            for k in range(PASSES):
                multiply(
                    base_banks[g][:], w_mx[k], slice(0, N), token_words[k][:, first:end],
                    token_scales[4 * k : P, first:end], k == 0, k == PASSES - 1,
                )

        def term_tile(g, name):
            return ring.tile([P, groups[g][1] - groups[g][0]], F32, name="%s%d" % (name, g), align_bytes=64)

        def window(r, g):
            return slot_results[:].indirect(token_slots[r][:, groups[g][0] // 16 : groups[g][1] // 16])

        def combine(g, name, a, b, op):
            total = term_tile(g, name)
            nc.vector.tensor_tensor(total[:], a, b, op)
            return total[:]

        picked = {}
        for g in range(2):
            for r in range(2):
                picked[r, g] = term_tile(g, "picked%d_" % r)
                nc.scalar.activation(picked[r, g][:], window(r, g), COPY)
        def weighted(r, g):
            return combine(g, "weighted%d_" % r, picked[r, g][:], gates[g][:, r, :], MULT)

        def fused(g):
            third = combine(g, "third", window(2, g), last_gate[:, slice(*groups[g])], MULT)
            return third

        def with_base(g, third):
            return combine(g, "with_base", third, base_banks[g][:], ADD)

        thirds = [fused(0), fused(1)]
        terms = [weighted(0, 0), weighted(1, 0)]
        terms.append(with_base(0, thirds[0]))
        blocks = FIRST_TOKENS // P
        turned_bank = psum.tile([P, blocks, P], F32, name=bank_tag(E - 1, 0))
        for i, term in enumerate(terms):
            for c in range(blocks):
                nc.tensor.matmul(
                    turned_bank[:, c, :], term[:, c * P : (c + 1) * P], identity[:], is_transpose=True,
                    start=i == 0 and c == 0, stop=i == len(terms) - 1 and c == blocks - 1,
                )
        turned = term_tile(0, "turned")
        move("S", turned[:], turned_bank[:].rearrange("p c n -> p (c n)"))
        back_bank = psum.tile([P, blocks, P], F32, name=bank_tag(E - 1, 1))
        for c in range(blocks):
            nc.tensor.transpose(back_bank[:, c, :], turned[:, c * P : (c + 1) * P], identity[:])
        total = term_tile(0, "total")
        move("S", total[:], back_bank[:].rearrange("p c n -> p (c n)"))
        nc.sync.dma_start(out=out[:, slice(*groups[0])], in_=total[:])

        first = weighted(0, 1)
        based = with_base(1, thirds[1])
        second = weighted(1, 1)
        partial = combine(1, "partial", first, based, ADD)
        total = combine(1, "total", partial, second, ADD)
        nc.sync.dma_start(out=out[:, slice(*groups[1])], in_=total)
